import numpy as np
CORES = [24,40,56,80,88,96]
N = 6
T, FF, CAP, CAPP = 4096, 4, 1056, 352
def entries(a): return a.T.reshape(-1)
def pack(v, P): return np.ascontiguousarray(np.asarray(v, np.int32).reshape(-1, P).T)
def lists(rng, how):
    O = np.stack([rng.permutation(np.repeat(np.arange(N), CAPP))[:CAP] for k in range(N)])
    if how == "apart": s = int(rng.integers(N * CAPP - CAP + 1)); cnt = np.bincount(np.repeat(np.arange(N), CAPP)[s:s + CAP], minlength=N); a = rng.permutation(N); O = np.stack([rng.permutation(np.repeat(np.arange(N), cnt[(a + k) % N])) for k in rng.permutation(N)])
    if how == "full": z = rng.permutation(N); O = np.stack([rng.permutation(np.repeat(z, CAPP)[:CAP]) for k in range(N)])
    if how == "none": z = int(rng.integers(N)); O = np.stack([rng.permutation(np.repeat(np.delete(np.arange(N), z), CAPP))[:CAP] for k in range(N)])
    P = np.zeros((N, CAP), np.int64)
    for o in range(N):
        q = rng.permutation(T); u = 0
        for k in range(N):
            m = np.nonzero(O[k] == o)[0]
            if how != "apart": q = rng.permutation(T); u = 0
            if how == "sorted": q = np.r_[0, T - 1, 1 + rng.permutation(T - 2)]
            P[k, m] = T * o + q[u:u + len(m)]; u += len(m)
    if how == "same": P = np.stack([rng.permutation(P[0]) for k in range(N)])
    if how == "sorted": P = np.sort(P, axis=1)
    G = 2 * rng.random((N, 16, CAP // 16), dtype=np.float32) - 1
    if how == "none": G[rng.random(G.shape) < 0.125] = 0
    return {"gate": G, "pick": np.stack([pack(p, 16) for p in P])}
def setup_inputs(rng):
    return dict({"x": rng.standard_normal((N, 128, T), dtype=np.float32), "w1": (rng.standard_normal((N, 128, FF * 128), dtype=np.float32) / 8), "w2": (rng.standard_normal((N, 128, FF * 128), dtype=np.float32) / 16)}, **lists(rng, "uniform"))
def setup_inputs_apart(rng):
    d = setup_inputs(rng); d.update(lists(rng, "apart"))
    for k in ("x",): d[k] = (d[k].astype(np.float32) * 1024.0).astype(d[k].dtype)
    return d
def setup_inputs_full(rng):
    d = setup_inputs(rng); d.update(lists(rng, "full"))
    for k in ("x",): d[k] = (d[k].astype(np.float32) * (1 / 1024.0)).astype(d[k].dtype)
    return d
def setup_inputs_none(rng):
    d = setup_inputs(rng); d.update(lists(rng, "none"))
    return d
def setup_inputs_same(rng):
    d = setup_inputs(rng); d.update(lists(rng, "same"))
    return d
def setup_inputs_sorted(rng):
    d = setup_inputs(rng); d.update(lists(rng, "sorted"))
    return d
def check_inputs(x):
    bad = []
    if x["pick"].min() < 0 or x["pick"].max() >= N * T: bad.append("pick out of range")
    if any(len(np.unique(a)) != a.size for a in x["pick"]): bad.append("a token stands twice in a list")
    if max(int(np.bincount(entries(a) // T, minlength=N).max()) for a in x["pick"]) > CAPP: bad.append("more than CAPP of an expert's tokens lie on one rank")
    return bad
def reference(x, w1, w2, gate, pick):
    X, W1, W2 = x.astype(np.float64), w1.astype(np.float64), w2.astype(np.float64)
    A = np.concatenate(list(X), axis=1); Y = np.zeros((128, N * T))
    for k in range(N):
        P = entries(pick[k]); g = entries(gate[k]).astype(np.float64)
        Y[:, P] += g[None, :] * sum(W2[k][:, 128 * f:128 * f + 128].T @ np.maximum(W1[k][:, 128 * f:128 * f + 128].T @ A[:, P], 0.0) for f in range(FF))
    return {"y": np.stack([Y[:, T * r:T * r + T] for r in range(N)]).astype(np.float32)}

@@ -1,0 +1,356 @@
+from concourse.bass import DstId, RemoteDMATransfer
+from concourse.mybir import AluOpType as A, ActivationFunctionType as F
+
+N, TOK, CAPP, CORES_SIM = 6, 4096, 352, 112
+NB = 4
+WB = 1024 // NB
+SL = CAPP // 16
+WIN = TOK + CAPP + 4
+CH = 9
+PARTS = [(0, 192), (192, 352)]
+XC = 4
+NT = 95
+XS = CAPP + 2 * SL
+
+_C9 = ["z9", "cl", "t2", "mk", "cum", "s1u", "s1", "cf", "af", "val"]
+_S = {
+    "pk": (12, "int32"), "L": (24, "float32"),
+    "ones": (128, "float32"), "tri": (128, "float32"), "ia": (128, "float32"), "ic": (SL, "float32"),
+    "c9": (12 * len(_C9), "float32"), "ci": (CH, "int32"), "pp": (2 * SL, "int32"), "pf2": (2 * SL, "float32"),
+    "padc": (2 * SL, "float32"), "lh": (CH * 128, "float32"), "rh": (CH * 2 * SL, "float32"), "msg": (2 * SL, "float32"),
+    "eoi": (SL, "int32"), "eo": (SL, "uint16"), "emi": (2 * CAPP, "int32"), "em": (CAPP, "float32"),
+    "xk": (XS, "float32"), "wsb": (1024, "float32"), "hid": (4 * CAPP, "float32"), "tmpg": (CAPP, "float32"),
+    "gs": (CAPP, "float32"), "res": (CAPP, "float32"),
+    "xw": (WIN, "float32"), "acc": (WIN, "float32"), "tmp": (N * CAPP, "float32"), "xs": (N * XS, "float32"),
+    "of": (N * SL, "uint16"), "land": (N * CAPP, "float32"),
+}
+SCRATCH = {n: ("sbuf", [128, c], d) for n, (c, d) in _S.items()}
+SCRATCH["wst"] = ("dram", [NB * 4, 128, WB // 4], "float32")
+SCRATCH["pc"] = ("dram", [NB, 128, WB // 4], "float32")
+SCRATCH["wland"] = ("dram", [NB * 4, 128, WB // 4], "float32")
+for _n in ("h0", "h1", "h2", "h3", "yb", "gb", "cb", "bb"):
+    SCRATCH[_n] = ("psum", [128, 512], "float32")
+SEMAPHORES = (["ls", "lst", "xin", "go0", "go1", "sum"] + ["pc%d" % b for b in range(NB)] + ["wa%d" % b for b in range(NB)]
+              + ["msg%d" % k for k in range(N)] + ["res%d_%d" % (k, h) for k in range(N) for h in range(len(PARTS))]
+              + ["t%d" % i for i in range(NT)])
+
+
+def _bits(m):
+    return [1 << i for i in range(16) if (m >> i) & 1]
+
+
+def _plan(s, cores, topo):
+    R = cores[s]
+    ch = topo.chip(R)
+    hel = [c for c in range(CORES_SIM) if topo.chip(c) == ch and c != R]
+    rot = [(s + i) % N for i in range(1, N)]
+    same = [r for r in rot if topo.same_plane(ch, topo.chip(cores[r]))]
+    cross = [r for r in rot if r not in same]
+    own = [c for c in hel if all(topo.may_write(c, cores[r]) for r in cross)]
+    rest = [c for c in hel if c not in own]
+    pack = dict(zip(cross + same, own + rest))
+    near = [c for c in hel if topo.die(c) == topo.die(R)] + [c for c in hel if topo.die(c) != topo.die(R)]
+    comp = dict(zip(cross + same, near))
+    return {"R": R, "hel": hel, "rot": rot, "same": same, "cross": cross, "own": own, "pack": pack, "comp": comp}
+
+
+def rank_program(g, core, T, topo):
+    cores = list(T.cores)
+    mine = [s for s in range(N) if topo.chip(cores[s]) == topo.chip(core)]
+    if not mine:
+        return
+    s = mine[0]
+    plans = [_plan(r, cores, topo) for r in range(N)]
+    P = plans[s]
+    R = P["R"]
+    is_rank = core == R
+    queues = {"v": g.vector, "a": g.scalar, "p": g.tensor, "g": g, "s": g.sync}
+    V = g.vector
+    count = [0]
+    waited = {}
+    nls = [0]
+
+    def tok(ins, n=1):
+        name = "t%d" % count[0]
+        count[0] += 1
+        ins.then_inc(T.sem[name], n)
+        return (name, n)
+
+    def need(q, *toks):
+        for name, n in toks:
+            if waited.get((q, name), 0) < n:
+                queues[q].wait_ge(T.sem[name], n)
+                waited[q, name] = n
+
+    def dst(c):
+        rid, pid, _ = topo.addr(c)
+        return DstId(rid=rid, pnc=pid)
+
+    def transfer(src, outs, sem, bits):
+        nls[0] += len(bits)
+        return RemoteDMATransfer(dst_ids=[dst(c) for c, _ in outs], dma_engine_mask=sum(bits), remote_sem=T.sem[sem],
+                                 srcs=[src], dsts=[o for _, o in outs])
+
+    def send(trs):
+        g.remote_dma_fused(trs, local_sem=T.sem.ls)
+
+    def wbits(c, b, to):
+        m = _bits(topo.mask(c, to))
+        return m[0::2] if b == 0 else m
+
+    def xs(k, a, b):
+        return T.xs[:, XS * k + a:XS * k + b]
+
+    def of(k, a=0, b=SL):
+        return T.of[:, SL * k + a:SL * k + b]
+
+    target = s if is_rank else None
+    for r, c in P["pack"].items():
+        if c == core:
+            target = r
+    expert = s if is_rank else None
+    for k, c in P["comp"].items():
+        if c == core:
+            expert = k
+
+    kc = {}
+    if is_rank:
+        m1 = tok(V.memset(T.pk[:, 8:9], -1))
+        m2 = tok(V.memset(T.L[:, 8:12], 0.0))
+        d1 = tok(g.sync.dma_start(T.pk[:, 0:8], T.pick[:, 0:64]), 16)
+        d3 = tok(g.scalar.dma_start(T.L[:, 0:8], T.gate[:, 0:64]), 16)
+        need("s", m1)
+        d2 = tok(g.sync.dma_start(T.pk[0:32, 8:9], T.pick[:, 64:66]), 16)
+        need("a", m2)
+        d4 = tok(g.scalar.dma_start(T.L[0:32, 8:9], T.gate[:, 64:66]), 16)
+        stg = []
+        for b in range(NB):
+            w = T.w1 if b < NB // 2 else T.w2
+            c0 = (b % (NB // 2)) * WB
+            stg.append(tok(g.sync.dma_start(T.wst[4 * b:4 * b + 4], w[:, c0:c0 + WB]), 16))
+        XW = TOK // XC
+        xl = []
+        for i in range(XC):
+            if i == 1:
+                g.sync.wait_ge(T.sem.go0, 1)
+            if i == 2:
+                g.sync.wait_ge(T.sem.go1, 1)
+            xl.append(tok(g.sync.dma_start(T.xw[:, XW * i:XW * i + XW], T.x[:, XW * i:XW * i + XW]), 16))
+        wl1 = tok(g.sync.dma_start(T.wsb[:, 0:512], T.w1[:]), 16)
+        wl2 = tok(g.sync.dma_start(T.wsb[:, 512:1024], T.w2[:]), 16)
+        wload = [wl1 if b < NB // 2 else wl2 for b in range(NB)]
+        xz = tok(V.memset(T.xw[:, TOK:WIN], 0.0))
+
+    c9 = {n: T.c9[:, 12 * i:12 * i + CH] for i, n in enumerate(_C9)}
+    if target is not None or expert is not None:
+        kc["o1"] = tok(V.memset(T.ones[:], 1.0))
+    if target is not None:
+        kc["z9"] = tok(V.memset(c9["z9"], 0.0))
+        pz = tok(V.memset(T.padc[:, 0:SL], 0.0))
+        if is_rank:
+            az = [tok(V.memset(T.acc[:, 0:1024], 0.0))]
+        need("g", kc["o1"])
+        kc["tri"] = tok(g.affine_select(T.tri[:], T.ones[:], [[1, 128]], A.is_gt, 0.0, 0, -1))
+        kc["ia"] = tok(g.iota(T.ia[:], [[0, 8], [1, 16]], 1, 0, allow_small_or_imprecise_dtypes=True))
+        kc["ic"] = tok(g.iota(T.ic[:], [[-16, SL]], 0, 0, allow_small_or_imprecise_dtypes=True))
+        kc["pp"] = tok(g.iota(T.pp[:, 0:SL], [[0, SL]], 0, 1))
+        kc["pcf"] = tok(g.iota(T.pf2[:, SL:2 * SL], [[16, SL]], TOK + 1, 0, allow_small_or_imprecise_dtypes=True))
+
+    if is_rank:
+        need("v", m1, d1, d2)
+        pfc = tok(V.tensor_copy(T.L[:, 12:21], T.pk[:, 0:CH]))
+        lists = [pfc, d3, d4, m2]
+        need("g", *lists)
+        hs = [P["pack"][r] for r in P["rot"]]
+        send([transfer(T.L[:, 0:21], [(c, T.L[:, 0:21]) for c in hs], "lst", _bits(topo.mask(core, hs[0])))])
+        for b in range(NB):
+            need("g", stg[b])
+            send([transfer(T.wst[4 * b + j], [(c, T.pc[b])], "pc%d" % b, _bits(topo.mask(core, c))[4 * j:4 * j + 4])
+                  for j, c in enumerate(P["own"])])
+            if b == 0:
+                g.sem_inc(T.sem.go0, 1)
+            if b == NB // 2 - 1:
+                g.sem_inc(T.sem.go1, 1)
+
+    if expert is not None:
+        kc["eoi"] = tok(g.iota(T.eoi[:], [[1, SL]], 0, 0))
+        kc["emi"] = tok(g.iota(T.emi[:, 0:CAPP], [[0, SL], [1, 16]], 128, -1))
+
+    def pad_constants():
+        need("v", kc["pp"])
+        q1 = tok(V.tensor_scalar(T.pp[:, SL:2 * SL], T.pp[:, 0:SL], 15, None, A.bitwise_and))
+        need("v", q1)
+        q2 = tok(V.tensor_copy(T.pf2[:, 0:SL], T.pp[:, SL:2 * SL]))
+        need("v", q2, kc["pcf"])
+        kc["padc"] = tok(V.tensor_tensor(T.padc[:, SL:2 * SL], T.pf2[:, 0:SL], T.pf2[:, SL:2 * SL], A.add))
+
+    def expert_constants():
+        need("v", kc["eoi"], kc["emi"])
+        kc["eo"] = tok(V.tensor_copy(T.eo[:], T.eoi[:]))
+        e1 = tok(V.tensor_scalar(T.emi[:, CAPP:2 * CAPP], T.emi[:, 0:CAPP], 15, None, A.bitwise_and))
+        need("v", e1)
+        kc["em"] = tok(V.tensor_scalar(T.em[:], T.emi[:, CAPP:2 * CAPP], 0.0, None, A.is_equal))
+
+    if target is not None:
+        pad_constants()
+    if expert is not None and not is_rank:
+        expert_constants()
+
+    def forward(b):
+        q = P["own"].index(core)
+        outs = [(plans[r]["comp"][s], T.wland[4 * b + q]) for r in P["rot"]]
+        g.wait_ge(T.sem["pc%d" % b], 4)
+        send([transfer(T.pc[b], outs, "wa%d" % b, wbits(core, b, outs[0][0]))])
+
+    if core in P["own"]:
+        forward(0)
+
+    if target is not None:
+        r = target
+        pf, gt = T.L[:, 12:21], T.L[:, 0:CH]
+        if is_rank:
+            need("v", *lists)
+        else:
+            V.wait_ge(T.sem.lst, len(_bits(topo.mask(R, core))))
+        a1 = tok(V.tensor_scalar(c9["cl"], pf, float(TOK * r), float(TOK * r + TOK - 1), A.max, A.min))
+        a2 = tok(V.tensor_scalar(c9["t2"], pf, float(-TOK * (r + 1)), None, A.add))
+        need("v", a1)
+        a3 = tok(V.tensor_tensor(c9["mk"], c9["cl"], pf, A.is_equal))
+        need("v", a3, kc["z9"])
+        a4 = tok(V.tensor_tensor_scan(c9["cum"], c9["mk"], c9["z9"], 0.0, A.add, A.add))
+        need("p", a4, kc["tri"])
+        a5 = tok(g.tensor.matmul(T.bb[:, 0:1], T.tri[:], c9["cum"][:, CH - 1:CH], True, True))
+        need("v", a4, a5)
+        a6 = tok(V.tensor_scalar(c9["s1u"], c9["cum"], T.bb[:, 0:1], None, A.add))
+        need("v", a6)
+        a7 = tok(V.tensor_tensor(c9["s1"], c9["s1u"], c9["mk"], A.mult))
+        need("v", a7)
+        a8 = tok(V.tensor_scalar(T.ci[:], c9["s1"], 1.0 / 16, 17.0 / 32, A.mult, A.subtract))
+        need("v", a2)
+        a9 = tok(V.tensor_tensor(c9["val"], c9["t2"], c9["s1"], A.subtract))
+        need("v", a8)
+        a10 = tok(V.tensor_scalar(c9["cf"], T.ci[:], -16.0, None, A.mult))
+        need("v", a10)
+        a11 = tok(V.tensor_tensor(c9["af"], c9["s1"], c9["cf"], A.add))
+        need("v", a9, a11, kc["ia"], kc["ic"])
+        for e in range(CH):
+            rh = T.rh[:, 2 * SL * e:2 * SL * e + SL]
+            rv = T.rh[:, 2 * SL * e + SL:2 * SL * e + 2 * SL]
+            lh = T.lh[:, 128 * e:128 * e + 128]
+            cfe = c9["cf"][:, e:e + 1]
+            b1 = tok(V.tensor_scalar(lh, T.ia[:], c9["af"][:, e:e + 1], None, A.is_equal))
+            V.tensor_scalar(rh, T.ic[:], cfe, gt[:, e:e + 1], A.is_equal, A.mult).then_inc(T.sem[b1[0]], 1)
+            V.tensor_scalar(rv, T.ic[:], cfe, c9["val"][:, e:e + 1], A.is_equal, A.mult).then_inc(T.sem[b1[0]], 1)
+            need("p", (b1[0], 3))
+            mm = g.tensor.matmul(T.cb[:, 0:2 * SL], lh, T.rh[:, 2 * SL * e:2 * SL * e + 2 * SL], e == 0, e == CH - 1)
+            if e == CH - 1:
+                cbt = tok(mm)
+        need("v", cbt, kc["padc"], pz)
+        mg = tok(V.tensor_tensor(xs(s, CAPP, XS) if is_rank else T.msg[:], T.cb[:, 0:2 * SL], T.padc[:], A.add))
+        if not is_rank:
+            need("g", mg)
+            hb = _bits(topo.mask(core, cores[r]))[1::2]
+            to = plans[r]["comp"][s]
+            send([transfer(T.msg[:], [(cores[r], xs(s, CAPP, XS)), (to, T.xk[:, CAPP:XS])], "msg%d" % s, hb)])
+
+    if core in P["own"]:
+        for b in range(1, NB):
+            forward(b)
+
+    order = P["same"] + P["cross"]
+    offs = {}
+
+    def offsets(k, deps):
+        need("v", *deps)
+        offs[k] = tok(V.tensor_copy(of(k), xs(k, CAPP + SL, XS)))
+
+    def gather(k):
+        need("v", offs[k], xz, *xl)
+        return tok(V.tensor_copy(xs(k, 0, CAPP), T.xw[:, 0:WIN].indirect(of(k))))
+
+    if is_rank:
+        expert_constants()
+        az.append(tok(V.memset(T.acc[:, 1024:WIN], 0.0)))
+        offsets(s, [mg])
+        for k in order:
+            c = P["comp"][k]
+            V.wait_ge(T.sem["msg%d" % k], 4)
+            offsets(k, [])
+            xg = gather(k)
+            need("g", xg)
+            send([transfer(xs(k, 0, CAPP), [(c, T.xk[:, 0:CAPP])], "xin", _bits(topo.mask(core, c)))])
+        xg = gather(s)
+
+    if expert is not None:
+        if is_rank:
+            xb = xs(s, 0, XS)
+            need("p", xg)
+            gsrc = xs(s, CAPP, CAPP + SL)
+            need("v", mg)
+        else:
+            xb = T.xk
+            gsrc = T.xk[:, CAPP:CAPP + SL]
+            wload = []
+            for b in range(NB):
+                tot = sum(len(wbits(c, b, core)) for c in plans[expert]["own"])
+                g.sync.wait_ge(T.sem["wa%d" % b], tot)
+                wload.append(tok(g.sync.dma_start(T.wsb[:, WB * b:WB * b + WB], T.wland[4 * b:4 * b + 4]), 16))
+            V.wait_ge(T.sem["msg%d" % expert], 4)
+        need("v", kc["eo"], kc["em"])
+        tg = tok(V.tensor_tensor(T.tmpg[:], gsrc.indirect(T.eo[:, 0:SL]), T.em[:], A.mult))
+        need("p", tg, kc["o1"])
+        gt_ = tok(g.tensor.matmul(T.gb[:, 0:CAPP], T.ones[0:16, 0:128], T.tmpg[0:16, :], True, True))
+        need("a", gt_)
+        gc = tok(g.scalar.activation(T.gs[:], T.gb[:, 0:CAPP], F.Copy))
+        if not is_rank:
+            g.tensor.wait_ge(T.sem.xin, len(_bits(topo.mask(R, core))))
+        hs = []
+        for f in range(4):
+            need("p", wload[128 * f // WB])
+            ht = tok(g.tensor.matmul(T["h%d" % f][:, 0:CAPP], T.wsb[:, 128 * f:128 * f + 128], xb[:, 0:CAPP], True, True))
+            need("a", ht)
+            hs.append(tok(g.scalar.activation(T.hid[:, CAPP * f:CAPP * f + CAPP], T["h%d" % f][:, 0:CAPP], F.Relu)))
+        rt = []
+        for h, (p0, p1) in enumerate(PARTS):
+            bank = [T.yb, T.bb][h]
+            for f in range(4):
+                need("p", wload[(512 + 128 * f) // WB], hs[f])
+                mm = g.tensor.matmul(bank[:, 0:p1 - p0], T.wsb[:, 512 + 128 * f:640 + 128 * f],
+                                     T.hid[:, CAPP * f + p0:CAPP * f + p1], f == 0, f == 3)
+                if f == 3:
+                    yt = tok(mm)
+            need("v", yt, gc)
+            rt.append(tok(V.tensor_tensor(T.res[:, p0:p1], bank[:, 0:p1 - p0], T.gs[:, p0:p1], A.mult)))
+            if not is_rank:
+                need("g", rt[h])
+                send([transfer(T.res[:, p0:p1], [(R, T.land[:, CAPP * expert + p0:CAPP * expert + p1])],
+                               "res%d_%d" % (expert, h), _bits(topo.mask(core, R)))])
+
+    if is_rank:
+        done = [0]
+
+        def step(ins):
+            ins.then_inc(T.sem.sum, 1)
+            done[0] += 1
+            V.wait_ge(T.sem.sum, done[0])
+
+        for h, (p0, p1) in enumerate(PARTS):
+            for k in [s] + order:
+                off = of(k, p0 // 16, p1 // 16)
+                if k == s:
+                    need("v", rt[h], *az)
+                    new = T.res[:, p0:p1]
+                else:
+                    V.wait_ge(T.sem["res%d_%d" % (k, h)], len(_bits(topo.mask(P["comp"][k], core))))
+                    new = T.land[:, CAPP * k + p0:CAPP * k + p1]
+                if k != s or h:
+                    t = T.tmp[:, CAPP * k + p0:CAPP * k + p1]
+                    step(V.tensor_tensor(t, T.acc[:].indirect(off), new, A.add))
+                    new = t
+                step(V.tensor_copy(T.acc[:].indirect(off), new))
+        g.sync.wait_ge(T.sem.sum, done[0])
+        yd = tok(g.sync.dma_start(T.y[:], T.acc[:, 0:TOK]), 16)
+        need("s", yd)
+
+    if nls[0]:
+        g.wait_ge(T.sem.ls, nls[0])

@@ -8,8 +8,11 @@ SL = CAPP // 16
 WIN = TOK + CAPP + 4
 CH = 9
 PARTS = [(0, 192), (192, 352)]
+SCAL = (3, 6, 8)
+RELAYED = 6
+SHARED = (1,)
 XC = 4
-NT = 95
+NT = 96
 XS = CAPP + 2 * SL
 
 _C9 = ["z9", "cl", "t2", "mk", "cum", "s1u", "s1", "cf", "af", "val"]
@@ -17,8 +20,9 @@ _S = {
     "pk": (12, "int32"), "L": (24, "float32"),
     "ones": (128, "float32"), "tri": (128, "float32"), "ia": (128, "float32"), "ic": (SL, "float32"),
     "c9": (12 * len(_C9), "float32"), "ci": (CH, "int32"), "pp": (2 * SL, "int32"), "pf2": (2 * SL, "float32"),
-    "padc": (2 * SL, "float32"), "lh": (CH * 128, "float32"), "rh": (CH * 2 * SL, "float32"), "msg": (2 * SL, "float32"),
-    "eoi": (SL, "int32"), "eo": (SL, "uint16"), "emi": (2 * CAPP, "int32"), "em": (CAPP, "float32"),
+    "padc": (2 * SL, "float32"), "lh": (CH * 128, "float32"), "dif": (CH * 128, "float32"),
+    "rh": (CH * 2 * SL, "float32"), "msg": (2 * SL, "float32"),
+    "eo": (SL, "uint16"), "em": (CAPP, "float32"),
     "xk": (XS, "float32"), "wsb": (1024, "float32"), "hid": (4 * CAPP, "float32"), "tmpg": (CAPP, "float32"),
     "gs": (CAPP, "float32"), "res": (CAPP, "float32"),
     "xw": (WIN, "float32"), "acc": (WIN, "float32"), "tmp": (N * CAPP, "float32"), "xs": (N * XS, "float32"),
@@ -27,16 +31,23 @@ _S = {
 SCRATCH = {n: ("sbuf", [128, c], d) for n, (c, d) in _S.items()}
 SCRATCH["wst"] = ("dram", [NB * 4, 128, WB // 4], "float32")
 SCRATCH["pc"] = ("dram", [NB, 128, WB // 4], "float32")
+SCRATCH["rl"] = ("dram", [N * NB, 128, WB // 4], "float32")
 SCRATCH["wland"] = ("dram", [NB * 4, 128, WB // 4], "float32")
 for _n in ("h0", "h1", "h2", "h3", "yb", "gb", "cb", "bb"):
     SCRATCH[_n] = ("psum", [128, 512], "float32")
-SEMAPHORES = (["ls", "lst", "xin", "go0", "go1", "sum"] + ["pc%d" % b for b in range(NB)] + ["wa%d" % b for b in range(NB)]
+SEMAPHORES = (["ls", "lst", "xin0", "xin1", "sum"] + ["go%d" % i for i in range(XC - 1)]
+              + ["pc%d" % b for b in range(NB)] + ["w%d_%d" % (k, b) for k in range(N) for b in range(NB)]
               + ["msg%d" % k for k in range(N)] + ["res%d_%d" % (k, h) for k in range(N) for h in range(len(PARTS))]
               + ["t%d" % i for i in range(NT)])
 
 
 def _bits(m):
     return [1 << i for i in range(16) if (m >> i) & 1]
+
+
+def _wbits(c, b, to, topo):
+    m = _bits(topo.mask(c, to))
+    return m[0::2] if b == 0 else m
 
 
 def _plan(s, cores, topo):
@@ -51,11 +62,57 @@ def _plan(s, cores, topo):
     pack = dict(zip(cross + same, own + rest))
     near = [c for c in hel if topo.die(c) == topo.die(R)] + [c for c in hel if topo.die(c) != topo.die(R)]
     comp = dict(zip(cross + same, near))
-    return {"R": R, "hel": hel, "rot": rot, "same": same, "cross": cross, "own": own, "pack": pack, "comp": comp}
+    stay = own.index([c for c in own if topo.die(c) == topo.die(R)][0])
+    fwd = {}
+    for b in range(NB):
+        taken = [q for q in range(4) if q != stay] if b in SHARED else []
+        for q, c in zip(taken, rest):
+            fwd[b, c] = (q, same)
+        for q, c in enumerate(own):
+            fwd[b, c] = (q, [r for r in rot if r in cross or q not in taken])
+    return {"R": R, "hel": hel, "rot": rot, "same": same, "cross": cross, "own": own, "pack": pack, "comp": comp,
+            "fwd": fwd}
+
+
+def _relays(r, cores, topo):
+    ch = topo.chip(cores[r])
+    return [c for c in range(CORES_SIM) if topo.mates(topo.chip(c), ch) and topo.may_write(c, cores[r])
+            and topo.chip(c) not in [topo.chip(x) for x in cores]]
+
+
+def _relay(c, s, b, r, cores, topo):
+    cross = _plan(r, cores, topo)["cross"]
+    if s not in cross or len(cross) * b + cross.index(s) >= RELAYED:
+        return None
+    peers = [x for x in _plan(s, cores, topo)["own"] if topo.die(x) == topo.die(c)]
+    there = [x for x in _relays(r, cores, topo) if topo.die(x) == topo.die(c)]
+    return there[peers.index(c)] if there else None
+
+
+def _relay_program(g, core, r, cores, T, topo):
+    n = 0
+    for b in range(NB):
+        for k in [(r - i) % N for i in range(1, N)]:
+            for q, c in enumerate(_plan(k, cores, topo)["own"]):
+                if _relay(c, k, b, r, cores, topo) != core:
+                    continue
+                to = _plan(r, cores, topo)["comp"][k]
+                sem = T.sem["w%d_%d" % (k, b)]
+                g.wait_ge(sem, len(_wbits(c, b, core, topo)))
+                rid, pid, _ = topo.addr(to)
+                bits = _bits(topo.mask(core, to))
+                g.remote_dma_fused([RemoteDMATransfer(
+                    dst_ids=[DstId(rid=rid, pnc=pid)], dma_engine_mask=sum(bits), remote_sem=sem,
+                    srcs=[T.rl[k * NB + b]], dsts=[T.wland[4 * b + q]])], local_sem=T.sem.ls)
+                n += len(bits)
+    g.wait_ge(T.sem.ls, n)
 
 
 def rank_program(g, core, T, topo):
     cores = list(T.cores)
+    for r in range(N):
+        if core in _relays(r, cores, topo):
+            return _relay_program(g, core, r, cores, T, topo)
     mine = [s for s in range(N) if topo.chip(cores[s]) == topo.chip(core)]
     if not mine:
         return
@@ -76,6 +133,10 @@ def rank_program(g, core, T, topo):
         ins.then_inc(T.sem[name], n)
         return (name, n)
 
+    def also(t, ins, n=1):
+        ins.then_inc(T.sem[t[0]], n)
+        return (t[0], t[1] + n)
+
     def need(q, *toks):
         for name, n in toks:
             if waited.get((q, name), 0) < n:
@@ -93,10 +154,6 @@ def rank_program(g, core, T, topo):
 
     def send(trs):
         g.remote_dma_fused(trs, local_sem=T.sem.ls)
-
-    def wbits(c, b, to):
-        m = _bits(topo.mask(c, to))
-        return m[0::2] if b == 0 else m
 
     def xs(k, a, b):
         return T.xs[:, XS * k + a:XS * k + b]
@@ -120,22 +177,20 @@ def rank_program(g, core, T, topo):
         d1 = tok(g.sync.dma_start(T.pk[:, 0:8], T.pick[:, 0:64]), 16)
         d3 = tok(g.scalar.dma_start(T.L[:, 0:8], T.gate[:, 0:64]), 16)
         need("s", m1)
-        d2 = tok(g.sync.dma_start(T.pk[0:32, 8:9], T.pick[:, 64:66]), 16)
+        d1 = also(d1, g.sync.dma_start(T.pk[0:32, 8:9], T.pick[:, 64:66]), 16)
         need("a", m2)
-        d4 = tok(g.scalar.dma_start(T.L[0:32, 8:9], T.gate[:, 64:66]), 16)
+        d3 = also(d3, g.scalar.dma_start(T.L[0:32, 8:9], T.gate[:, 64:66]), 16)
         stg = []
         for b in range(NB):
             w = T.w1 if b < NB // 2 else T.w2
             c0 = (b % (NB // 2)) * WB
             stg.append(tok(g.sync.dma_start(T.wst[4 * b:4 * b + 4], w[:, c0:c0 + WB]), 16))
         XW = TOK // XC
-        xl = []
         for i in range(XC):
-            if i == 1:
-                g.sync.wait_ge(T.sem.go0, 1)
-            if i == 2:
-                g.sync.wait_ge(T.sem.go1, 1)
-            xl.append(tok(g.sync.dma_start(T.xw[:, XW * i:XW * i + XW], T.x[:, XW * i:XW * i + XW]), 16))
+            if i:
+                g.sync.wait_ge(T.sem["go%d" % (i - 1)], 1)
+            ins = g.sync.dma_start(T.xw[:, XW * i:XW * i + XW], T.x[:, XW * i:XW * i + XW])
+            xl = also(xl, ins, 16) if i else tok(ins, 16)
         wl1 = tok(g.sync.dma_start(T.wsb[:, 0:512], T.w1[:]), 16)
         wl2 = tok(g.sync.dma_start(T.wsb[:, 512:1024], T.w2[:]), 16)
         wload = [wl1 if b < NB // 2 else wl2 for b in range(NB)]
@@ -146,64 +201,75 @@ def rank_program(g, core, T, topo):
         kc["o1"] = tok(V.memset(T.ones[:], 1.0))
     if target is not None:
         kc["z9"] = tok(V.memset(c9["z9"], 0.0))
-        pz = tok(V.memset(T.padc[:, 0:SL], 0.0))
         if is_rank:
             az = [tok(V.memset(T.acc[:, 0:1024], 0.0))]
         need("g", kc["o1"])
         kc["tri"] = tok(g.affine_select(T.tri[:], T.ones[:], [[1, 128]], A.is_gt, 0.0, 0, -1))
-        kc["ia"] = tok(g.iota(T.ia[:], [[0, 8], [1, 16]], 1, 0, allow_small_or_imprecise_dtypes=True))
-        kc["ic"] = tok(g.iota(T.ic[:], [[-16, SL]], 0, 0, allow_small_or_imprecise_dtypes=True))
+    if target is not None or expert is not None:
         kc["pp"] = tok(g.iota(T.pp[:, 0:SL], [[0, SL]], 0, 1))
-        kc["pcf"] = tok(g.iota(T.pf2[:, SL:2 * SL], [[16, SL]], TOK + 1, 0, allow_small_or_imprecise_dtypes=True))
+        kc["ic"] = tok(g.iota(T.ic[:], [[-16, SL]], 0, 0, allow_small_or_imprecise_dtypes=True))
+        kc["ia"] = tok(g.iota(T.ia[:], [[0, 8], [1, 16]], 1, 0, allow_small_or_imprecise_dtypes=True))
+
+    def pieces(b):
+        hs = [c for c in P["hel"] if (b, c) in P["fwd"]]
+        return hs, (4 if len(hs) <= 4 else 2)
 
     if is_rank:
-        need("v", m1, d1, d2)
+        need("v", m1, d1)
         pfc = tok(V.tensor_copy(T.L[:, 12:21], T.pk[:, 0:CH]))
-        lists = [pfc, d3, d4, m2]
+        lists = [pfc, d3, m2]
         need("g", *lists)
         hs = [P["pack"][r] for r in P["rot"]]
         send([transfer(T.L[:, 0:21], [(c, T.L[:, 0:21]) for c in hs], "lst", _bits(topo.mask(core, hs[0])))])
         for b in range(NB):
             need("g", stg[b])
-            send([transfer(T.wst[4 * b + j], [(c, T.pc[b])], "pc%d" % b, _bits(topo.mask(core, c))[4 * j:4 * j + 4])
-                  for j, c in enumerate(P["own"])])
-            if b == 0:
-                g.sem_inc(T.sem.go0, 1)
-            if b == NB // 2 - 1:
-                g.sem_inc(T.sem.go1, 1)
-
-    if expert is not None:
-        kc["eoi"] = tok(g.iota(T.eoi[:], [[1, SL]], 0, 0))
-        kc["emi"] = tok(g.iota(T.emi[:, 0:CAPP], [[0, SL], [1, 16]], 128, -1))
+            hs, ne = pieces(b)
+            send([transfer(T.wst[4 * b + P["fwd"][b, c][0]], [(c, T.pc[b])], "pc%d" % b,
+                           _bits(topo.mask(core, c))[ne * j:ne * j + ne]) for j, c in enumerate(hs)])
+            if b < XC - 1:
+                g.sem_inc(T.sem["go%d" % b], 1)
 
     def pad_constants():
-        need("v", kc["pp"])
+        need("v", kc["pp"], kc["ic"])
         q1 = tok(V.tensor_scalar(T.pp[:, SL:2 * SL], T.pp[:, 0:SL], 15, None, A.bitwise_and))
         need("v", q1)
-        q2 = tok(V.tensor_copy(T.pf2[:, 0:SL], T.pp[:, SL:2 * SL]))
-        need("v", q2, kc["pcf"])
-        kc["padc"] = tok(V.tensor_tensor(T.padc[:, SL:2 * SL], T.pf2[:, 0:SL], T.pf2[:, SL:2 * SL], A.add))
+        kc["pm"] = tok(V.tensor_copy(T.pf2[:, 0:SL], T.pp[:, SL:2 * SL]))
+        need("v", kc["pm"])
+        if target is not None:
+            q3 = tok(V.tensor_scalar(T.padc[:, 0:SL], T.ic[:], -1.0, float(TOK + 1), A.mult, A.add))
+            need("v", q3)
+            q4 = tok(V.tensor_tensor(T.padc[:, SL:2 * SL], T.pf2[:, 0:SL], T.padc[:, 0:SL], A.add))
+            need("v", q4)
+            kc["padc"] = tok(V.memset(T.padc[:, 0:SL], 0.0))
 
     def expert_constants():
-        need("v", kc["eoi"], kc["emi"])
-        kc["eo"] = tok(V.tensor_copy(T.eo[:], T.eoi[:]))
-        e1 = tok(V.tensor_scalar(T.emi[:, CAPP:2 * CAPP], T.emi[:, 0:CAPP], 15, None, A.bitwise_and))
+        need("v", kc["ic"], kc["ia"], kc["pm"])
+        kc["eo"] = tok(V.tensor_scalar(T.eo[:], T.ic[:], -1.0 / 16, None, A.mult))
+        e1 = tok(V.tensor_scalar(T.pf2[:, SL:SL + 1], T.pf2[:, 0:1], 1.0, None, A.add))
         need("v", e1)
-        kc["em"] = tok(V.tensor_scalar(T.em[:], T.emi[:, CAPP:2 * CAPP], 0.0, None, A.is_equal))
+        for c in range(0, CAPP, 128):
+            w = min(128, CAPP - c)
+            ins = V.tensor_scalar(T.em[:, c:c + w], T.ia[:, 0:w], T.pf2[:, SL:SL + 1], None, A.is_equal)
+            kc["em"] = also(kc["em"], ins) if c else tok(ins)
 
-    if target is not None:
+    if target is not None or expert is not None:
         pad_constants()
     if expert is not None and not is_rank:
         expert_constants()
 
-    def forward(b):
-        q = P["own"].index(core)
-        outs = [(plans[r]["comp"][s], T.wland[4 * b + q]) for r in P["rot"]]
-        g.wait_ge(T.sem["pc%d" % b], 4)
-        send([transfer(T.pc[b], outs, "wa%d" % b, wbits(core, b, outs[0][0]))])
+    def forward(blocks):
+        for b in blocks:
+            if (b, core) not in P["fwd"]:
+                continue
+            q, ranks = P["fwd"][b, core]
+            via = {r: _relay(core, s, b, r, cores, topo) for r in ranks}
+            outs = ([(via[r], T.rl[s * NB + b]) for r in ranks if via[r] is not None]
+                    + [(plans[r]["comp"][s], T.wland[4 * b + q]) for r in ranks if via[r] is None])
+            g.wait_ge(T.sem["pc%d" % b], pieces(b)[1])
+            send([transfer(T.pc[b], outs, "w%d_%d" % (s, b), _wbits(core, b, outs[0][0], topo))])
 
-    if core in P["own"]:
-        forward(0)
+    first = 1 if core in P["own"] else NB
+    forward(range(first))
 
     if target is not None:
         r = target
@@ -237,92 +303,104 @@ def rank_program(g, core, T, topo):
             rh = T.rh[:, 2 * SL * e:2 * SL * e + SL]
             rv = T.rh[:, 2 * SL * e + SL:2 * SL * e + 2 * SL]
             lh = T.lh[:, 128 * e:128 * e + 128]
-            cfe = c9["cf"][:, e:e + 1]
-            b1 = tok(V.tensor_scalar(lh, T.ia[:], c9["af"][:, e:e + 1], None, A.is_equal))
-            V.tensor_scalar(rh, T.ic[:], cfe, gt[:, e:e + 1], A.is_equal, A.mult).then_inc(T.sem[b1[0]], 1)
-            V.tensor_scalar(rv, T.ic[:], cfe, c9["val"][:, e:e + 1], A.is_equal, A.mult).then_inc(T.sem[b1[0]], 1)
-            need("p", (b1[0], 3))
+            cfe, afe = c9["cf"][:, e:e + 1], c9["af"][:, e:e + 1]
+            b1 = tok(V.tensor_scalar(rh, T.ic[:], cfe, gt[:, e:e + 1], A.is_equal, A.mult))
+            if e in SCAL:
+                dif = T.dif[:, 128 * e:128 * e + 128]
+                need("a", a11, kc["ia"])
+                need("a", tok(g.scalar.activation(dif, T.ia[:], F.Abs, afe, -1.0)))
+                b1 = also(b1, g.scalar.activation(lh, dif, F.Relu, 1.0, -1.0))
+            else:
+                b1 = also(b1, V.tensor_scalar(lh, T.ia[:], afe, None, A.is_equal))
+            b1 = also(b1, V.tensor_scalar(rv, T.ic[:], cfe, c9["val"][:, e:e + 1], A.is_equal, A.mult))
+            need("p", b1)
             mm = g.tensor.matmul(T.cb[:, 0:2 * SL], lh, T.rh[:, 2 * SL * e:2 * SL * e + 2 * SL], e == 0, e == CH - 1)
             if e == CH - 1:
                 cbt = tok(mm)
-        need("v", cbt, kc["padc"], pz)
+        need("v", cbt, kc["padc"])
         mg = tok(V.tensor_tensor(xs(s, CAPP, XS) if is_rank else T.msg[:], T.cb[:, 0:2 * SL], T.padc[:], A.add))
         if not is_rank:
             need("g", mg)
-            hb = _bits(topo.mask(core, cores[r]))[1::2]
             to = plans[r]["comp"][s]
-            send([transfer(T.msg[:], [(cores[r], xs(s, CAPP, XS)), (to, T.xk[:, CAPP:XS])], "msg%d" % s, hb)])
+            send([transfer(T.msg[:], [(cores[r], xs(s, CAPP, XS)), (to, T.xk[:, CAPP:XS])], "msg%d" % s,
+                           _bits(topo.mask(core, cores[r])))])
 
-    if core in P["own"]:
-        for b in range(1, NB):
-            forward(b)
+    def packed(k):
+        V.wait_ge(T.sem["msg%d" % k], len(_bits(topo.mask(plans[k]["pack"][s], R))))
 
-    order = P["same"] + P["cross"]
+    forward(range(first, NB))
+
+    def factors(src):
+        need("v", kc["eo"], kc["em"])
+        tg = tok(V.tensor_tensor(T.tmpg[:], src.indirect(T.eo[:, 0:SL]), T.em[:], A.mult))
+        need("p", tg, kc["o1"])
+        gm = tok(g.tensor.matmul(T.gb[:, 0:CAPP], T.ones[0:16, 0:128], T.tmpg[0:16, :], True, True))
+        need("a", gm)
+        return tok(g.scalar.activation(T.gs[:], T.gb[:, 0:CAPP], F.Copy))
+
+    order = P["same"][::-1] + P["cross"][::-1]
     offs = {}
 
-    def offsets(k, deps):
-        need("v", *deps)
+    def offsets(k):
         offs[k] = tok(V.tensor_copy(of(k), xs(k, CAPP + SL, XS)))
 
-    def gather(k):
-        need("v", offs[k], xz, *xl)
-        return tok(V.tensor_copy(xs(k, 0, CAPP), T.xw[:, 0:WIN].indirect(of(k))))
+    def gather(k, q, p0, p1):
+        need(q, offs[k], xz, xl)
+        src = T.xw[:, 0:WIN].indirect(of(k, p0 // 16, p1 // 16))
+        return tok(V.tensor_copy(xs(k, p0, p1), src) if q == "v" else g.scalar.activation(xs(k, p0, p1), src, F.Copy))
 
     if is_rank:
         expert_constants()
         az.append(tok(V.memset(T.acc[:, 1024:WIN], 0.0)))
-        offsets(s, [mg])
-        for k in order:
-            c = P["comp"][k]
-            V.wait_ge(T.sem["msg%d" % k], 4)
-            offsets(k, [])
-            xg = gather(k)
-            need("g", xg)
-            send([transfer(xs(k, 0, CAPP), [(c, T.xk[:, 0:CAPP])], "xin", _bits(topo.mask(core, c)))])
-        xg = gather(s)
+        need("v", mg)
+        offsets(s)
+        gc = factors(xs(s, CAPP, CAPP + SL))
+        xown = gather(s, "v", 0, CAPP)
+        for h, (p0, p1) in enumerate(PARTS):
+            for i, k in enumerate(order):
+                if h == 0:
+                    packed(k)
+                    offsets(k)
+                need("g", gather(k, "av"[i % 2], p0, p1))
+                c = P["comp"][k]
+                send([transfer(xs(k, p0, p1), [(c, T.xk[:, p0:p1])], "xin%d" % h, _bits(topo.mask(core, c)))])
 
     if expert is not None:
         if is_rank:
             xb = xs(s, 0, XS)
-            need("p", xg)
-            gsrc = xs(s, CAPP, CAPP + SL)
-            need("v", mg)
+            need("p", xown)
         else:
             xb = T.xk
-            gsrc = T.xk[:, CAPP:CAPP + SL]
             wload = []
             for b in range(NB):
-                tot = sum(len(wbits(c, b, core)) for c in plans[expert]["own"])
-                g.sync.wait_ge(T.sem["wa%d" % b], tot)
+                tot = 0
+                for (b2, c), (q, ranks) in plans[expert]["fwd"].items():
+                    if b2 == b and s in ranks:
+                        v = _relay(c, expert, b, s, cores, topo)
+                        tot += len(_wbits(c, b, core, topo)) if v is None else len(_bits(topo.mask(v, core)))
+                g.sync.wait_ge(T.sem["w%d_%d" % (expert, b)], tot)
                 wload.append(tok(g.sync.dma_start(T.wsb[:, WB * b:WB * b + WB], T.wland[4 * b:4 * b + 4]), 16))
-            V.wait_ge(T.sem["msg%d" % expert], 4)
-        need("v", kc["eo"], kc["em"])
-        tg = tok(V.tensor_tensor(T.tmpg[:], gsrc.indirect(T.eo[:, 0:SL]), T.em[:], A.mult))
-        need("p", tg, kc["o1"])
-        gt_ = tok(g.tensor.matmul(T.gb[:, 0:CAPP], T.ones[0:16, 0:128], T.tmpg[0:16, :], True, True))
-        need("a", gt_)
-        gc = tok(g.scalar.activation(T.gs[:], T.gb[:, 0:CAPP], F.Copy))
-        if not is_rank:
-            g.tensor.wait_ge(T.sem.xin, len(_bits(topo.mask(R, core))))
-        hs = []
-        for f in range(4):
-            need("p", wload[128 * f // WB])
-            ht = tok(g.tensor.matmul(T["h%d" % f][:, 0:CAPP], T.wsb[:, 128 * f:128 * f + 128], xb[:, 0:CAPP], True, True))
-            need("a", ht)
-            hs.append(tok(g.scalar.activation(T.hid[:, CAPP * f:CAPP * f + CAPP], T["h%d" % f][:, 0:CAPP], F.Relu)))
-        rt = []
+            packed(expert)
+            gc = factors(T.xk[:, CAPP:CAPP + SL])
+        ybank = [T.yb, T.bb]
+        yt = []
         for h, (p0, p1) in enumerate(PARTS):
-            bank = [T.yb, T.bb][h]
+            if not is_rank:
+                g.tensor.wait_ge(T.sem["xin%d" % h], len(_bits(topo.mask(R, core))))
+            hs = []
+            for f in range(4):
+                need("p", wload[128 * f // WB])
+                ht = tok(g.tensor.matmul(T["h%d" % f][:, p0:p1], T.wsb[:, 128 * f:128 * f + 128], xb[:, p0:p1], True, True))
+                need("a", ht)
+                hs.append(tok(g.scalar.activation(T.hid[:, CAPP * f + p0:CAPP * f + p1], T["h%d" % f][:, p0:p1], F.Relu)))
             for f in range(4):
                 need("p", wload[(512 + 128 * f) // WB], hs[f])
-                mm = g.tensor.matmul(bank[:, 0:p1 - p0], T.wsb[:, 512 + 128 * f:640 + 128 * f],
+                mm = g.tensor.matmul(ybank[h][:, 0:p1 - p0], T.wsb[:, 512 + 128 * f:640 + 128 * f],
                                      T.hid[:, CAPP * f + p0:CAPP * f + p1], f == 0, f == 3)
-                if f == 3:
-                    yt = tok(mm)
-            need("v", yt, gc)
-            rt.append(tok(V.tensor_tensor(T.res[:, p0:p1], bank[:, 0:p1 - p0], T.gs[:, p0:p1], A.mult)))
+            yt.append(tok(mm))
             if not is_rank:
-                need("g", rt[h])
+                need("v", yt[h], gc)
+                need("g", tok(V.tensor_tensor(T.res[:, p0:p1], ybank[h][:, 0:p1 - p0], T.gs[:, p0:p1], A.mult)))
                 send([transfer(T.res[:, p0:p1], [(R, T.land[:, CAPP * expert + p0:CAPP * expert + p1])],
                                "res%d_%d" % (expert, h), _bits(topo.mask(core, R)))])
 
@@ -338,8 +416,9 @@ def rank_program(g, core, T, topo):
             for k in [s] + order:
                 off = of(k, p0 // 16, p1 // 16)
                 if k == s:
-                    need("v", rt[h], *az)
+                    need("v", yt[h], gc, *az)
                     new = T.res[:, p0:p1]
+                    step(V.tensor_tensor(new, ybank[h][:, 0:p1 - p0], T.gs[:, p0:p1], A.mult))
                 else:
                     V.wait_ge(T.sem["res%d_%d" % (k, h)], len(_bits(topo.mask(P["comp"][k], core))))
                     new = T.land[:, CAPP * k + p0:CAPP * k + p1]

@@ -12,8 +12,13 @@ SCAL = (3, 6, 8)
 RELAYED = 6
 SHARED = (1,)
 XC = 4
-NT = 96
+NT = 94
 XS = CAPP + 2 * SL
+Z0 = 4
+ROW = 280
+SETS = [(0, 32), (32, 64), (64, 128)]
+YP = [(0, 256, "v"), (256, 768, "a"), (768, 1280, "v"), (1280, 2048, "a"), (2048, 2816, "v"), (2816, 3456, "a"),
+      (3456, 4096, "v")]
 
 _C9 = ["z9", "cl", "t2", "mk", "cum", "s1u", "s1", "cf", "af", "val"]
 _S = {
@@ -25,29 +30,30 @@ _S = {
     "eo": (SL, "uint16"), "em": (CAPP, "float32"),
     "xk": (XS, "float32"), "wsb": (1024, "float32"), "hid": (4 * CAPP, "float32"), "tmpg": (CAPP, "float32"),
     "gs": (CAPP, "float32"), "res": (CAPP, "float32"),
-    "xw": (WIN, "float32"), "acc": (WIN, "float32"), "tmp": (N * CAPP, "float32"), "xs": (N * XS, "float32"),
-    "of": (N * SL, "uint16"), "land": (N * CAPP, "float32"),
+    "win": (16 * ROW, "float32"), "ids": (CAPP, "float32"), "idt": (N * CAPP, "float32"), "rm": (CAPP, "float32"),
+    "pg": (CAPP, "float32"), "ps": (CAPP, "float32"), "pv": (SL, "uint16"), "oq": (SL, "uint16"),
+    "oi": (N * SL, "int32"), "oh": (N * SL, "int32"), "oa": (N * SL, "float32"), "ob": (N * SL, "float32"),
+    "oc": (N * SL, "float32"), "op": (2 * SL, "uint16"), "iv": (3 * ROW, "float32"), "im": (512, "float32"),
+    "xw": (WIN, "float32"), "yb": (TOK, "float32"), "xs": (N * XS, "float32"),
+    "of": (N * SL, "uint16"), "pvl": (N * SL, "uint16"), "inv": (256, "uint16"),
+    "land": (Z0 + N * CAPP, "float32"),
 }
 SCRATCH = {n: ("sbuf", [128, c], d) for n, (c, d) in _S.items()}
 SCRATCH["wst"] = ("dram", [NB * 4, 128, WB // 4], "float32")
 SCRATCH["pc"] = ("dram", [NB, 128, WB // 4], "float32")
-SCRATCH["rl"] = ("dram", [N * NB, 128, WB // 4], "float32")
+SCRATCH["rl"] = ("dram", [RELAYED, 128, WB // 4], "float32")
 SCRATCH["wland"] = ("dram", [NB * 4, 128, WB // 4], "float32")
-for _n in ("h0", "h1", "h2", "h3", "yb", "gb", "cb", "bb"):
+for _n in ("h0", "h1", "h2", "h3", "y0", "gb", "cb", "bb"):
     SCRATCH[_n] = ("psum", [128, 512], "float32")
-SEMAPHORES = (["ls", "lst", "xin0", "xin1", "sum"] + ["go%d" % i for i in range(XC - 1)]
-              + ["pc%d" % b for b in range(NB)] + ["w%d_%d" % (k, b) for k in range(N) for b in range(NB)]
-              + ["msg%d" % k for k in range(N)] + ["res%d_%d" % (k, h) for k in range(N) for h in range(len(PARTS))]
-              + ["t%d" % i for i in range(NT)])
+SEMAPHORES = (["ls", "lst", "xin", "sum", "lk"] + ["go%d" % i for i in range(XC - 1)]
+              + ["%s%d" % (n, b) for n in ("pc", "wx") for b in range(NB)]
+              + ["w%d_%d" % (i, b) for i in range(4) for b in range(NB)]
+              + ["msg%d" % k for k in range(N)] + ["of%d" % i for i in range(3)] + ["pv%d" % q for q in range(1, N)]
+              + ["res%d_%d" % (q, h) for q in range(1, N) for h in range(len(PARTS))] + ["t%d" % i for i in range(NT)])
 
 
 def _bits(m):
     return [1 << i for i in range(16) if (m >> i) & 1]
-
-
-def _wbits(c, b, to, topo):
-    m = _bits(topo.mask(c, to))
-    return m[0::2] if b == 0 else m
 
 
 def _plan(s, cores, topo):
@@ -62,6 +68,12 @@ def _plan(s, cores, topo):
     pack = dict(zip(cross + same, own + rest))
     near = [c for c in hel if topo.die(c) == topo.die(R)] + [c for c in hel if topo.die(c) != topo.die(R)]
     comp = dict(zip(cross + same, near))
+    spare = [c for c in hel if c not in comp.values()]
+    soon = [r for r in cross if topo.mates(ch, topo.chip(cores[r]))] + same[::-1]
+    share = dict(zip(soon, spare))
+    whole = [r for r in soon[::-1] + cross[::-1] if r not in share]
+    order = whole + list(share)
+    add = list(share) + whole
     stay = own.index([c for c in own if topo.die(c) == topo.die(R)][0])
     fwd = {}
     for b in range(NB):
@@ -71,7 +83,17 @@ def _plan(s, cores, topo):
         for q, c in enumerate(own):
             fwd[b, c] = (q, [r for r in rot if r in cross or q not in taken])
     return {"R": R, "hel": hel, "rot": rot, "same": same, "cross": cross, "own": own, "pack": pack, "comp": comp,
-            "fwd": fwd}
+            "fwd": fwd, "order": order, "share": share, "add": add}
+
+
+def _wsem(k, b, cores, topo):
+    kin = [x for x in range(N) if x == k or topo.same_plane(topo.chip(cores[x]), topo.chip(cores[k]))]
+    return "w%d_%d" % (kin.index(k), b)
+
+
+def _wbits(c, b, to, topo):
+    m = _bits(topo.mask(c, to))
+    return m[0::2] if b == 0 else m
 
 
 def _relays(r, cores, topo):
@@ -80,44 +102,45 @@ def _relays(r, cores, topo):
             and topo.chip(c) not in [topo.chip(x) for x in cores]]
 
 
-def _relay(c, s, b, r, cores, topo):
-    cross = _plan(r, cores, topo)["cross"]
-    if s not in cross or len(cross) * b + cross.index(s) >= RELAYED:
+def _relay(c, s, b, r, plans, cores, topo):
+    cross = plans[r]["cross"]
+    if s not in cross or c not in plans[s]["own"] or len(cross) * b + cross.index(s) >= RELAYED:
         return None
-    peers = [x for x in _plan(s, cores, topo)["own"] if topo.die(x) == topo.die(c)]
+    peers = [x for x in plans[s]["own"] if topo.die(x) == topo.die(c)]
     there = [x for x in _relays(r, cores, topo) if topo.die(x) == topo.die(c)]
-    return there[peers.index(c)] if there else None
+    return (there[peers.index(c)], len(cross) * b + cross.index(s)) if there else None
 
 
-def _relay_program(g, core, r, cores, T, topo):
+def _relay_program(g, core, r, plans, cores, T, topo):
     n = 0
     for b in range(NB):
         for k in [(r - i) % N for i in range(1, N)]:
-            for q, c in enumerate(_plan(k, cores, topo)["own"]):
-                if _relay(c, k, b, r, cores, topo) != core:
+            for q, c in enumerate(plans[k]["own"]):
+                via = _relay(c, k, b, r, plans, cores, topo)
+                if via is None or via[0] != core:
                     continue
-                to = _plan(r, cores, topo)["comp"][k]
-                sem = T.sem["w%d_%d" % (k, b)]
+                to = plans[r]["comp"][k]
+                sem = T.sem[_wsem(k, b, cores, topo)]
                 g.wait_ge(sem, len(_wbits(c, b, core, topo)))
                 rid, pid, _ = topo.addr(to)
                 bits = _bits(topo.mask(core, to))
                 g.remote_dma_fused([RemoteDMATransfer(
                     dst_ids=[DstId(rid=rid, pnc=pid)], dma_engine_mask=sum(bits), remote_sem=sem,
-                    srcs=[T.rl[k * NB + b]], dsts=[T.wland[4 * b + q]])], local_sem=T.sem.ls)
+                    srcs=[T.rl[via[1]]], dsts=[T.wland[4 * b + q]])], local_sem=T.sem.ls)
                 n += len(bits)
     g.wait_ge(T.sem.ls, n)
 
 
 def rank_program(g, core, T, topo):
     cores = list(T.cores)
-    for r in range(N):
-        if core in _relays(r, cores, topo):
-            return _relay_program(g, core, r, cores, T, topo)
+    relay_of = [r for r in range(N) if core in _relays(r, cores, topo)]
     mine = [s for s in range(N) if topo.chip(cores[s]) == topo.chip(core)]
-    if not mine:
+    if not mine and not relay_of:
         return
-    s = mine[0]
     plans = [_plan(r, cores, topo) for r in range(N)]
+    if relay_of:
+        return _relay_program(g, core, relay_of[0], plans, cores, T, topo)
+    s = mine[0]
     P = plans[s]
     R = P["R"]
     is_rank = core == R
@@ -126,6 +149,9 @@ def rank_program(g, core, T, topo):
     count = [0]
     waited = {}
     nls = [0]
+    steps = [0]
+    chip_bits = _bits(topo.mask(R, P["hel"][0]))
+    nof = len(chip_bits)
 
     def tok(ins, n=1):
         name = "t%d" % count[0]
@@ -143,6 +169,12 @@ def rank_program(g, core, T, topo):
                 queues[q].wait_ge(T.sem[name], n)
                 waited[q, name] = n
 
+    def step(ins, wait=True):
+        ins.then_inc(T.sem.lk, 1)
+        steps[0] += 1
+        if wait:
+            V.wait_ge(T.sem.lk, steps[0])
+
     def dst(c):
         rid, pid, _ = topo.addr(c)
         return DstId(rid=rid, pnc=pid)
@@ -155,20 +187,30 @@ def rank_program(g, core, T, topo):
     def send(trs):
         g.remote_dma_fused(trs, local_sem=T.sem.ls)
 
+    order = P["order"]
+    place = dict([(s, 0)] + [(k, 1 + i) for i, k in enumerate(P["add"])])
+
     def xs(k, a, b):
         return T.xs[:, XS * k + a:XS * k + b]
 
-    def of(k, a=0, b=SL):
-        return T.of[:, SL * k + a:SL * k + b]
+    def of(k):
+        return T.of[:, SL * place[k]:SL * place[k] + SL]
 
-    target = s if is_rank else None
-    for r, c in P["pack"].items():
-        if c == core:
-            target = r
-    expert = s if is_rank else None
-    for k, c in P["comp"].items():
-        if c == core:
-            expert = k
+    def land(q, a, b):
+        return T.land[:, Z0 + CAPP * q + a:Z0 + CAPP * q + b]
+
+    def key(table):
+        return [k for k, c in table.items() if c == core]
+
+    target = s if is_rank else (key(P["pack"]) + [None])[0]
+    second = (key(P["share"]) + [None])[0]
+    expert = s if is_rank else (key(P["comp"]) + [second])[0]
+    lead = not is_rank and expert is not None and second is None
+    other = P["share"].get(expert) if lead else None
+    parts = [] if expert is None else [1] if second is not None else [0] if other is not None else [0, 1]
+    lo, hi = (PARTS[parts[0]][0], PARTS[parts[-1]][1]) if parts else (0, 0)
+    n_sh = 1 + len(P["share"])
+    told = [(0, 1), (1, n_sh), (n_sh, N - 1)]
 
     kc = {}
     if is_rank:
@@ -197,18 +239,18 @@ def rank_program(g, core, T, topo):
         xz = tok(V.memset(T.xw[:, TOK:WIN], 0.0))
 
     c9 = {n: T.c9[:, 12 * i:12 * i + CH] for i, n in enumerate(_C9)}
-    if target is not None or expert is not None:
-        kc["o1"] = tok(V.memset(T.ones[:], 1.0))
+    kc["o1"] = tok(V.memset(T.ones[:], 1.0))
     if target is not None:
         kc["z9"] = tok(V.memset(c9["z9"], 0.0))
         if is_rank:
-            az = [tok(V.memset(T.acc[:, 0:1024], 0.0))]
+            wz = tok(V.memset(T.win[:, 0:1024], 0.0))
         need("g", kc["o1"])
         kc["tri"] = tok(g.affine_select(T.tri[:], T.ones[:], [[1, 128]], A.is_gt, 0.0, 0, -1))
-    if target is not None or expert is not None:
-        kc["pp"] = tok(g.iota(T.pp[:, 0:SL], [[0, SL]], 0, 1))
-        kc["ic"] = tok(g.iota(T.ic[:], [[-16, SL]], 0, 0, allow_small_or_imprecise_dtypes=True))
-        kc["ia"] = tok(g.iota(T.ia[:], [[0, 8], [1, 16]], 1, 0, allow_small_or_imprecise_dtypes=True))
+    kc["pp"] = tok(g.iota(T.pp[:, 0:SL], [[0, SL]], 0, 1))
+    kc["ic"] = tok(g.iota(T.ic[:], [[-16, SL]], 0, 0, allow_small_or_imprecise_dtypes=True))
+    kc["ia"] = tok(g.iota(T.ia[:], [[0, 8], [1, 16]], 1, 0, allow_small_or_imprecise_dtypes=True))
+    if lead:
+        kc["ids"] = tok(g.iota(T.ids[:], [[1, CAPP]], Z0, 0, allow_small_or_imprecise_dtypes=True))
 
     def pieces(b):
         hs = [c for c in P["hel"] if (b, c) in P["fwd"]]
@@ -220,14 +262,21 @@ def rank_program(g, core, T, topo):
         lists = [pfc, d3, m2]
         need("g", *lists)
         hs = [P["pack"][r] for r in P["rot"]]
-        send([transfer(T.L[:, 0:21], [(c, T.L[:, 0:21]) for c in hs], "lst", _bits(topo.mask(core, hs[0])))])
+        send([transfer(T.L[:, 0:21], [(c, T.L[:, 0:21]) for c in hs], "lst", chip_bits)])
         for b in range(NB):
             need("g", stg[b])
             hs, ne = pieces(b)
             send([transfer(T.wst[4 * b + P["fwd"][b, c][0]], [(c, T.pc[b])], "pc%d" % b,
-                           _bits(topo.mask(core, c))[ne * j:ne * j + ne]) for j, c in enumerate(hs)])
+                           chip_bits[ne * j:ne * j + ne]) for j, c in enumerate(hs)])
             if b < XC - 1:
                 g.sem_inc(T.sem["go%d" % b], 1)
+        need("g", kc["tri"], kc["pp"], kc["ic"], kc["ia"])
+        for i in range(2):
+            for a, (p0, p1) in enumerate(SETS):
+                ins = g.iota(T.idt[p0:p1, CAPP * i:CAPP * i + CAPP], [[1, CAPP]], Z0 + CAPP * (3 * i + a), 0,
+                             allow_small_or_imprecise_dtypes=True)
+                idt = also(idt, ins) if i or a else tok(ins)
+                need("g", idt)
 
     def pad_constants():
         need("v", kc["pp"], kc["ic"])
@@ -252,9 +301,8 @@ def rank_program(g, core, T, topo):
             ins = V.tensor_scalar(T.em[:, c:c + w], T.ia[:, 0:w], T.pf2[:, SL:SL + 1], None, A.is_equal)
             kc["em"] = also(kc["em"], ins) if c else tok(ins)
 
-    if target is not None or expert is not None:
-        pad_constants()
-    if expert is not None and not is_rank:
+    pad_constants()
+    if parts and not is_rank:
         expert_constants()
 
     def forward(blocks):
@@ -262,11 +310,11 @@ def rank_program(g, core, T, topo):
             if (b, core) not in P["fwd"]:
                 continue
             q, ranks = P["fwd"][b, core]
-            via = {r: _relay(core, s, b, r, cores, topo) for r in ranks}
-            outs = ([(via[r], T.rl[s * NB + b]) for r in ranks if via[r] is not None]
+            via = {r: _relay(core, s, b, r, plans, cores, topo) for r in ranks}
+            outs = ([(via[r][0], T.rl[via[r][1]]) for r in ranks if via[r] is not None]
                     + [(plans[r]["comp"][s], T.wland[4 * b + q]) for r in ranks if via[r] is None])
             g.wait_ge(T.sem["pc%d" % b], pieces(b)[1])
-            send([transfer(T.pc[b], outs, "w%d_%d" % (s, b), _wbits(core, b, outs[0][0], topo))])
+            send([transfer(T.pc[b], outs, _wsem(s, b, cores, topo), _wbits(core, b, outs[0][0], topo))])
 
     first = 1 if core in P["own"] else NB
     forward(range(first))
@@ -277,7 +325,7 @@ def rank_program(g, core, T, topo):
         if is_rank:
             need("v", *lists)
         else:
-            V.wait_ge(T.sem.lst, len(_bits(topo.mask(R, core))))
+            V.wait_ge(T.sem.lst, nof)
         a1 = tok(V.tensor_scalar(c9["cl"], pf, float(TOK * r), float(TOK * r + TOK - 1), A.max, A.min))
         a2 = tok(V.tensor_scalar(c9["t2"], pf, float(-TOK * (r + 1)), None, A.add))
         need("v", a1)
@@ -330,105 +378,192 @@ def rank_program(g, core, T, topo):
 
     forward(range(first, NB))
 
+    if lead:
+        me = place[expert]
+        wz = tok(V.memset(T.win[:, 0:WIN], 0.0))
+        need("v", kc["ids"], kc["ia"])
+        for q in range(1, me):
+            ins = V.tensor_scalar(T.idt[:, CAPP * q:CAPP * q + CAPP], T.ids[:], float(CAPP * q), None, A.add)
+            idt = also(idt, ins) if q > 1 else tok(ins)
+        for c in range(0, CAPP, 128):
+            w = min(128, CAPP - c)
+            ins = V.tensor_scalar(T.rm[:, c:c + w], T.ia[:, 0:w], 1.0, None, A.is_gt)
+            kc["rm"] = also(kc["rm"], ins) if c else tok(ins)
+
     def factors(src):
         need("v", kc["eo"], kc["em"])
-        tg = tok(V.tensor_tensor(T.tmpg[:], src.indirect(T.eo[:, 0:SL]), T.em[:], A.mult))
+        tg = tok(V.tensor_tensor(T.tmpg[:, lo:hi], src.indirect(T.eo[:, lo // 16:hi // 16]), T.em[:, lo:hi], A.mult))
         need("p", tg, kc["o1"])
-        gm = tok(g.tensor.matmul(T.gb[:, 0:CAPP], T.ones[0:16, 0:128], T.tmpg[0:16, :], True, True))
+        gm = tok(g.tensor.matmul(T.gb[:, lo:hi], T.ones[0:16, 0:128], T.tmpg[0:16, lo:hi], True, True))
         need("a", gm)
-        return tok(g.scalar.activation(T.gs[:], T.gb[:, 0:CAPP], F.Copy))
-
-    order = P["same"][::-1] + P["cross"][::-1]
-    offs = {}
-
-    def offsets(k):
-        offs[k] = tok(V.tensor_copy(of(k), xs(k, CAPP + SL, XS)))
-
-    def gather(k, q, p0, p1):
-        need(q, offs[k], xz, xl)
-        src = T.xw[:, 0:WIN].indirect(of(k, p0 // 16, p1 // 16))
-        return tok(V.tensor_copy(xs(k, p0, p1), src) if q == "v" else g.scalar.activation(xs(k, p0, p1), src, F.Copy))
+        return tok(g.scalar.activation(T.gs[:, lo:hi], T.gb[:, lo:hi], F.Copy))
 
     if is_rank:
+        offs = {}
+
+        def offsets(k):
+            offs[k] = tok(V.tensor_copy(of(k), xs(k, CAPP + SL, XS)))
+
+        def tell(i):
+            q0, q1 = told[i]
+            hs = [P["comp"][x] for x in order if place[x] > q0]
+            need("g", *[offs[k] for k in offs if q0 <= place[k] < q1])
+            lot = T.of[:, SL * q0:SL * q1]
+            send([transfer(lot, [(c, lot) for c in hs], "of%d" % i, chip_bits)])
+
+        def gather(k, q):
+            need(q, offs[k], xz, xl)
+            src = T.xw[:, 0:WIN].indirect(of(k))
+            return tok(V.tensor_copy(xs(k, 0, CAPP), src) if q == "v"
+                       else g.scalar.activation(xs(k, 0, CAPP), src, F.Copy))
+
         expert_constants()
-        az.append(tok(V.memset(T.acc[:, 1024:WIN], 0.0)))
+        zz = tok(V.memset(T.land[:, 0:Z0], 0.0))
         need("v", mg)
         offsets(s)
+        tell(0)
         gc = factors(xs(s, CAPP, CAPP + SL))
-        xown = gather(s, "v", 0, CAPP)
-        for h, (p0, p1) in enumerate(PARTS):
-            for i, k in enumerate(order):
-                if h == 0:
-                    packed(k)
-                    offsets(k)
-                need("g", gather(k, "av"[i % 2], p0, p1))
-                c = P["comp"][k]
-                send([transfer(xs(k, p0, p1), [(c, T.xk[:, p0:p1])], "xin%d" % h, _bits(topo.mask(core, c)))])
+        wz = also(wz, V.memset(T.win[:, 1024:16 * ROW], 0.0))
+        xown = gather(s, "v")
+        half = XS - PARTS[1][0]
+        for i, k in enumerate(order):
+            packed(k)
+            offsets(k)
+            need("g", gather(k, "av"[i % 2]))
+            c = P["comp"][k]
+            if k in P["share"]:
+                send([transfer(xs(k, 0, half), [(c, T.xk[:, 0:half])], "xin", chip_bits[:nof // 2]),
+                      transfer(xs(k, XS - half, XS), [(P["share"][k], T.xk[:, XS - half:XS])], "xin",
+                               chip_bits[nof // 2:])])
+            else:
+                send([transfer(xs(k, 0, CAPP), [(c, T.xk[:, 0:CAPP])], "xin", chip_bits)])
+            if k == order[-1]:
+                tell(1)
+            elif i == N - 2 - len(P["share"]):
+                tell(2)
+        need("v", *offs.values())
+        step(V.tensor_copy(T.oi[:], T.of[:]))
+        step(V.tensor_scalar(T.oh[:], T.oi[:], 4, None, A.arith_shift_right))
+        step(V.tensor_scalar(T.oa[:], T.oi[:], float(ROW), None, A.mult), False)
+        step(V.tensor_scalar(T.ob[:], T.oh[:], float(1 - 16 * ROW), None, A.mult))
+        step(V.tensor_tensor(T.oc[:], T.oa[:], T.ob[:], A.add))
+        for i in range(2):
+            for a, (p0, p1) in enumerate(SETS):
+                step(V.tensor_copy(T.op[p0:p1, SL * i:SL * i + SL],
+                                   T.oc[p0:p1, SL * (3 * i + a):SL * (3 * i + a + 1)]), i == 1 and a == 2)
+        need("v", idt, wz)
+        for i in range(2):
+            step(V.tensor_copy(T.win[:].indirect(T.op[:, SL * i:SL * i + SL]), T.idt[:, CAPP * i:CAPP * i + CAPP]))
+        g.sync.wait_ge(T.sem.lk, steps[0])
+        for a in range(3):
+            ins = g.sync.dma_start(T.iv[:, ROW * a:ROW * a + ROW], T.win[32 * a:32 * a + 8, :])
+            ivt = also(ivt, ins, 16) if a else tok(ins, 16)
 
-    if expert is not None:
-        if is_rank:
-            xb = xs(s, 0, XS)
-            need("p", xown)
-        else:
-            xb = T.xk
-            wload = []
-            for b in range(NB):
-                tot = 0
-                for (b2, c), (q, ranks) in plans[expert]["fwd"].items():
-                    if b2 == b and s in ranks:
-                        v = _relay(c, expert, b, s, cores, topo)
-                        tot += len(_wbits(c, b, core, topo)) if v is None else len(_bits(topo.mask(v, core)))
-                g.sync.wait_ge(T.sem["w%d_%d" % (expert, b)], tot)
-                wload.append(tok(g.sync.dma_start(T.wsb[:, WB * b:WB * b + WB], T.wland[4 * b:4 * b + 4]), 16))
-            packed(expert)
-            gc = factors(T.xk[:, CAPP:CAPP + SL])
-        ybank = [T.yb, T.bb]
-        yt = []
-        for h, (p0, p1) in enumerate(PARTS):
-            if not is_rank:
-                g.tensor.wait_ge(T.sem["xin%d" % h], len(_bits(topo.mask(R, core))))
-            hs = []
-            for f in range(4):
-                need("p", wload[128 * f // WB])
-                ht = tok(g.tensor.matmul(T["h%d" % f][:, p0:p1], T.wsb[:, 128 * f:128 * f + 128], xb[:, p0:p1], True, True))
-                need("a", ht)
-                hs.append(tok(g.scalar.activation(T.hid[:, CAPP * f + p0:CAPP * f + p1], T["h%d" % f][:, p0:p1], F.Relu)))
-            for f in range(4):
-                need("p", wload[(512 + 128 * f) // WB], hs[f])
-                mm = g.tensor.matmul(ybank[h][:, 0:p1 - p0], T.wsb[:, 512 + 128 * f:640 + 128 * f],
-                                     T.hid[:, CAPP * f + p0:CAPP * f + p1], f == 0, f == 3)
-            yt.append(tok(mm))
-            if not is_rank:
-                need("v", yt[h], gc)
-                need("g", tok(V.tensor_tensor(T.res[:, p0:p1], ybank[h][:, 0:p1 - p0], T.gs[:, p0:p1], A.mult)))
-                send([transfer(T.res[:, p0:p1], [(R, T.land[:, CAPP * expert + p0:CAPP * expert + p1])],
-                               "res%d_%d" % (expert, h), _bits(topo.mask(core, R)))])
+    def make_prev():
+        need("v", wz, kc["ids"])
+        for q in range(me):
+            for i, (q0, _) in enumerate(told):
+                if q0 == q:
+                    V.wait_ge(T.sem["of%d" % i], nof)
+            if q:
+                need("v", idt)
+            ids = T.idt[:, CAPP * q:CAPP * q + CAPP] if q else T.ids[:]
+            need("v", tok(V.tensor_copy(T.win[:, 0:WIN].indirect(T.of[:, SL * q:SL * q + SL]), ids)))
+        need("v", oq, kc["em"], kc["rm"])
+        p1 = tok(V.tensor_tensor(T.pg[:], T.win[:, 0:WIN].indirect(T.oq[:, 0:SL]), T.em[:], A.mult))
+        need("v", p1)
+        p2 = tok(V.tensor_tensor_scan(T.ps[:], T.rm[:], T.pg[:], 0.0, A.mult, A.add))
+        need("v", p2)
+        need("g", tok(V.tensor_copy(T.pv[:], T.ps[:, 15:CAPP:16])))
+        send([transfer(T.pv[:], [(R, T.pvl[:, SL * me:SL * me + SL])], "pv%d" % me, chip_bits)])
+
+    def first_layer():
+        hs = []
+        for f in range(4):
+            need("p", wload[128 * f // WB])
+            ht = tok(g.tensor.matmul(T["h%d" % f][:, lo:hi], T.wsb[:, 128 * f:128 * f + 128], xb[:, lo:hi], True, True))
+            need("a", ht)
+            hs.append(tok(g.scalar.activation(T.hid[:, CAPP * f + lo:CAPP * f + hi], T["h%d" % f][:, lo:hi], F.Relu)))
+        return hs
 
     if is_rank:
-        done = [0]
+        xb = xs(s, 0, XS)
+        need("p", xown)
+        hid = first_layer()
+    elif lead:
+        xb = T.xk
+        wload = []
+        for b in range(NB):
+            tot = 0
+            for (b2, c), (q, ranks) in plans[expert]["fwd"].items():
+                if b2 == b and s in ranks:
+                    v = _relay(c, expert, b, s, plans, cores, topo)
+                    tot += len(_wbits(c, b, core, topo)) if v is None else len(_bits(topo.mask(v[0], core)))
+            g.sync.wait_ge(T.sem[_wsem(expert, b, cores, topo)], tot)
+            wload.append(tok(g.sync.dma_start(T.wsb[:, WB * b:WB * b + WB], T.wland[4 * b:4 * b + 4]), 16))
+            if other is not None:
+                need("g", wload[b])
+                send([transfer(T.wsb[:, WB * b:WB * b + WB], [(other, T.wsb[:, WB * b:WB * b + WB])], "wx%d" % b,
+                               chip_bits)])
+        packed(expert)
+        oq = tok(V.tensor_copy(T.oq[:], T.xk[:, CAPP + SL:XS]))
+        gc = factors(T.xk[:, CAPP:CAPP + SL])
+        make_prev()
+        g.tensor.wait_ge(T.sem.xin, nof if other is None else nof // 2)
+        hid = first_layer()
+    elif second is not None:
+        xb = T.xk
+        wload = [("wx%d" % b, nof) for b in range(NB)]
+        g.tensor.wait_ge(T.sem.xin, nof // 2)
+        hid = first_layer()
+        V.wait_ge(T.sem.xin, nof // 2)
+        gc = factors(T.xk[:, CAPP:CAPP + SL])
+    ybank = [T.y0, T.bb]
+    yt = {}
+    for f in range(4 if parts else 0):
+        need("p", wload[(512 + 128 * f) // WB], hid[f])
+        for h in parts:
+            p0, p1 = PARTS[h]
+            mm = g.tensor.matmul(ybank[h][:, 0:p1 - p0], T.wsb[:, 512 + 128 * f:640 + 128 * f],
+                                 T.hid[:, CAPP * f + p0:CAPP * f + p1], f == 0, f == 3)
+            if f == 3:
+                yt[h] = tok(mm)
+    for h in parts:
+        p0, p1 = PARTS[h]
+        need("v", yt[h], gc)
+        if is_rank:
+            own_res = V.tensor_tensor(land(0, p0, p1), ybank[h][:, 0:p1 - p0], T.gs[:, p0:p1], A.mult)
+            ownt = also(ownt, own_res) if h else tok(own_res)
+        else:
+            need("g", tok(V.tensor_tensor(T.res[:, p0:p1], ybank[h][:, 0:p1 - p0], T.gs[:, p0:p1], A.mult)))
+            send([transfer(T.res[:, p0:p1], [(R, land(place[expert], p0, p1))],
+                           "res%d_%d" % (place[expert], h), chip_bits)])
 
-        def step(ins):
-            ins.then_inc(T.sem.sum, 1)
-            done[0] += 1
-            V.wait_ge(T.sem.sum, done[0])
-
-        for h, (p0, p1) in enumerate(PARTS):
-            for k in [s] + order:
-                off = of(k, p0 // 16, p1 // 16)
-                if k == s:
-                    need("v", yt[h], gc, *az)
-                    new = T.res[:, p0:p1]
-                    step(V.tensor_tensor(new, ybank[h][:, 0:p1 - p0], T.gs[:, p0:p1], A.mult))
-                else:
-                    V.wait_ge(T.sem["res%d_%d" % (k, h)], len(_bits(topo.mask(P["comp"][k], core))))
-                    new = T.land[:, CAPP * k + p0:CAPP * k + p1]
-                if k != s or h:
-                    t = T.tmp[:, CAPP * k + p0:CAPP * k + p1]
-                    step(V.tensor_tensor(t, T.acc[:].indirect(off), new, A.add))
-                    new = t
-                step(V.tensor_copy(T.acc[:].indirect(off), new))
-        g.sync.wait_ge(T.sem.sum, done[0])
-        yd = tok(g.sync.dma_start(T.y[:], T.acc[:, 0:TOK]), 16)
+    if is_rank:
+        need("v", ivt)
+        step(V.tensor_tensor(T.im[:, 0:256], T.iv[:, 0:256], T.iv[:, ROW:ROW + 256], A.max))
+        step(V.tensor_tensor(T.im[:, 256:512], T.im[:, 0:256], T.iv[:, 2 * ROW:2 * ROW + 256], A.max))
+        step(V.tensor_copy(T.inv[:], T.im[:, 256:512]))
+        n = 0
+        need("v", zz, ownt)
+        for q in range(1, N):
+            V.wait_ge(T.sem["pv%d" % q], nof)
+            for h, (p0, p1) in enumerate(PARTS):
+                V.wait_ge(T.sem["res%d_%d" % (q, h)], nof)
+                off = T.pvl[:, SL * q + p0 // 16:SL * q + p1 // 16]
+                V.tensor_tensor(land(q, p0, p1), T.land[:, 0:Z0 + CAPP * q].indirect(off), land(q, p0, p1),
+                                A.add).then_inc(T.sem.sum, 1)
+                n += 1
+            V.wait_ge(T.sem.sum, n)
+        g.scalar.wait_ge(T.sem.sum, n)
+        g.scalar.wait_ge(T.sem.lk, steps[0])
+        yd = None
+        for a, b, q in YP:
+            src = T.land[:].indirect(T.inv[:, a // 16:b // 16])
+            need("s", tok(V.tensor_copy(T.yb[:, a:b], src) if q == "v"
+                          else g.scalar.activation(T.yb[:, a:b], src, F.Copy)))
+            ins = g.sync.dma_start(T.y[:, a:b], T.yb[:, a:b])
+            yd = also(yd, ins, 16) if yd else tok(ins, 16)
         need("s", yd)
 
     if nls[0]:

from concourse.bass import DstId, RemoteDMATransfer
from concourse.mybir import AluOpType as A, ActivationFunctionType as F

N, TOK, CAPP, CORES_SIM = 6, 4096, 352, 112
NB = 4
WB = 1024 // NB
SL = CAPP // 16
WIN = TOK + CAPP + 4
CH = 9
PARTS = [(0, 192), (192, 352)]
SCAL = (3, 6, 8)
RELAYED = 6
SHARED = (1,)
XC = 4
NT = 94
XS = CAPP + 2 * SL
Z0 = 4
ROW = 280
SETS = [(0, 32), (32, 64), (64, 128)]
YP = [(0, 256, "v"), (256, 768, "a"), (768, 1280, "v"), (1280, 2048, "a"), (2048, 2816, "v"), (2816, 3456, "a"),
      (3456, 4096, "v")]

_C9 = ["z9", "cl", "t2", "mk", "cum", "s1u", "s1", "cf", "af", "val"]
_S = {
    "pk": (12, "int32"), "L": (24, "float32"),
    "ones": (128, "float32"), "tri": (128, "float32"), "ia": (128, "float32"), "ic": (SL, "float32"),
    "c9": (12 * len(_C9), "float32"), "ci": (CH, "int32"), "pp": (2 * SL, "int32"), "pf2": (2 * SL, "float32"),
    "padc": (2 * SL, "float32"), "lh": (CH * 128, "float32"), "dif": (CH * 128, "float32"),
    "rh": (CH * 2 * SL, "float32"), "msg": (2 * SL, "float32"),
    "eo": (SL, "uint16"), "em": (CAPP, "float32"),
    "xk": (XS, "float32"), "wsb": (1024, "float32"), "hid": (4 * CAPP, "float32"), "tmpg": (CAPP, "float32"),
    "gs": (CAPP, "float32"), "res": (CAPP, "float32"),
    "win": (16 * ROW, "float32"), "ids": (CAPP, "float32"), "idt": (N * CAPP, "float32"), "rm": (CAPP, "float32"),
    "pg": (CAPP, "float32"), "ps": (CAPP, "float32"), "pv": (SL, "uint16"), "oq": (SL, "uint16"),
    "oi": (N * SL, "int32"), "oh": (N * SL, "int32"), "oa": (N * SL, "float32"), "ob": (N * SL, "float32"),
    "oc": (N * SL, "float32"), "op": (2 * SL, "uint16"), "iv": (3 * ROW, "float32"), "im": (512, "float32"),
    "xw": (WIN, "float32"), "yb": (TOK, "float32"), "xs": (N * XS, "float32"),
    "of": (N * SL, "uint16"), "pvl": (N * SL, "uint16"), "inv": (256, "uint16"),
    "land": (Z0 + N * CAPP, "float32"),
}
SCRATCH = {n: ("sbuf", [128, c], d) for n, (c, d) in _S.items()}
SCRATCH["wst"] = ("dram", [NB * 4, 128, WB // 4], "float32")
SCRATCH["pc"] = ("dram", [NB, 128, WB // 4], "float32")
SCRATCH["rl"] = ("dram", [RELAYED, 128, WB // 4], "float32")
SCRATCH["wland"] = ("dram", [NB * 4, 128, WB // 4], "float32")
for _n in ("h0", "h1", "h2", "h3", "y0", "gb", "cb", "bb"):
    SCRATCH[_n] = ("psum", [128, 512], "float32")
SEMAPHORES = (["ls", "lst", "xin", "sum", "lk"] + ["go%d" % i for i in range(XC - 1)]
              + ["%s%d" % (n, b) for n in ("pc", "wx") for b in range(NB)]
              + ["w%d_%d" % (i, b) for i in range(4) for b in range(NB)]
              + ["msg%d" % k for k in range(N)] + ["of%d" % i for i in range(3)] + ["pv%d" % q for q in range(1, N)]
              + ["res%d_%d" % (q, h) for q in range(1, N) for h in range(len(PARTS))] + ["t%d" % i for i in range(NT)])


def _bits(m):
    return [1 << i for i in range(16) if (m >> i) & 1]


def _plan(s, cores, topo):
    R = cores[s]
    ch = topo.chip(R)
    hel = [c for c in range(CORES_SIM) if topo.chip(c) == ch and c != R]
    rot = [(s + i) % N for i in range(1, N)]
    same = [r for r in rot if topo.same_plane(ch, topo.chip(cores[r]))]
    cross = [r for r in rot if r not in same]
    own = [c for c in hel if all(topo.may_write(c, cores[r]) for r in cross)]
    rest = [c for c in hel if c not in own]
    pack = dict(zip(cross + same, own + rest))
    near = [c for c in hel if topo.die(c) == topo.die(R)] + [c for c in hel if topo.die(c) != topo.die(R)]
    comp = dict(zip(cross + same, near))
    spare = [c for c in hel if c not in comp.values()]
    soon = [r for r in cross if topo.mates(ch, topo.chip(cores[r]))] + same[::-1]
    share = dict(zip(soon, spare))
    whole = [r for r in soon[::-1] + cross[::-1] if r not in share]
    order = whole + list(share)
    add = list(share) + whole
    stay = own.index([c for c in own if topo.die(c) == topo.die(R)][0])
    fwd = {}
    for b in range(NB):
        taken = [q for q in range(4) if q != stay] if b in SHARED else []
        for q, c in zip(taken, rest):
            fwd[b, c] = (q, same)
        for q, c in enumerate(own):
            fwd[b, c] = (q, [r for r in rot if r in cross or q not in taken])
    return {"R": R, "hel": hel, "rot": rot, "same": same, "cross": cross, "own": own, "pack": pack, "comp": comp,
            "fwd": fwd, "order": order, "share": share, "add": add}


def _wsem(k, b, cores, topo):
    kin = [x for x in range(N) if x == k or topo.same_plane(topo.chip(cores[x]), topo.chip(cores[k]))]
    return "w%d_%d" % (kin.index(k), b)


def _wbits(c, b, to, topo):
    m = _bits(topo.mask(c, to))
    return m[0::2] if b == 0 else m


def _relays(r, cores, topo):
    ch = topo.chip(cores[r])
    return [c for c in range(CORES_SIM) if topo.mates(topo.chip(c), ch) and topo.may_write(c, cores[r])
            and topo.chip(c) not in [topo.chip(x) for x in cores]]


def _relay(c, s, b, r, plans, cores, topo):
    cross = plans[r]["cross"]
    if s not in cross or c not in plans[s]["own"] or len(cross) * b + cross.index(s) >= RELAYED:
        return None
    peers = [x for x in plans[s]["own"] if topo.die(x) == topo.die(c)]
    there = [x for x in _relays(r, cores, topo) if topo.die(x) == topo.die(c)]
    return (there[peers.index(c)], len(cross) * b + cross.index(s)) if there else None


def _relay_program(g, core, r, plans, cores, T, topo):
    n = 0
    for b in range(NB):
        for k in [(r - i) % N for i in range(1, N)]:
            for q, c in enumerate(plans[k]["own"]):
                via = _relay(c, k, b, r, plans, cores, topo)
                if via is None or via[0] != core:
                    continue
                to = plans[r]["comp"][k]
                sem = T.sem[_wsem(k, b, cores, topo)]
                g.wait_ge(sem, len(_wbits(c, b, core, topo)))
                rid, pid, _ = topo.addr(to)
                bits = _bits(topo.mask(core, to))
                g.remote_dma_fused([RemoteDMATransfer(
                    dst_ids=[DstId(rid=rid, pnc=pid)], dma_engine_mask=sum(bits), remote_sem=sem,
                    srcs=[T.rl[via[1]]], dsts=[T.wland[4 * b + q]])], local_sem=T.sem.ls)
                n += len(bits)
    g.wait_ge(T.sem.ls, n)


def rank_program(g, core, T, topo):
    cores = list(T.cores)
    relay_of = [r for r in range(N) if core in _relays(r, cores, topo)]
    mine = [s for s in range(N) if topo.chip(cores[s]) == topo.chip(core)]
    if not mine and not relay_of:
        return
    plans = [_plan(r, cores, topo) for r in range(N)]
    if relay_of:
        return _relay_program(g, core, relay_of[0], plans, cores, T, topo)
    s = mine[0]
    P = plans[s]
    R = P["R"]
    is_rank = core == R
    queues = {"v": g.vector, "a": g.scalar, "p": g.tensor, "g": g, "s": g.sync}
    V = g.vector
    count = [0]
    waited = {}
    nls = [0]
    steps = [0]
    chip_bits = _bits(topo.mask(R, P["hel"][0]))
    nof = len(chip_bits)

    def tok(ins, n=1):
        name = "t%d" % count[0]
        count[0] += 1
        ins.then_inc(T.sem[name], n)
        return (name, n)

    def also(t, ins, n=1):
        ins.then_inc(T.sem[t[0]], n)
        return (t[0], t[1] + n)

    def need(q, *toks):
        for name, n in toks:
            if waited.get((q, name), 0) < n:
                queues[q].wait_ge(T.sem[name], n)
                waited[q, name] = n

    def step(ins, wait=True):
        ins.then_inc(T.sem.lk, 1)
        steps[0] += 1
        if wait:
            V.wait_ge(T.sem.lk, steps[0])

    def dst(c):
        rid, pid, _ = topo.addr(c)
        return DstId(rid=rid, pnc=pid)

    def transfer(src, outs, sem, bits):
        nls[0] += len(bits)
        return RemoteDMATransfer(dst_ids=[dst(c) for c, _ in outs], dma_engine_mask=sum(bits), remote_sem=T.sem[sem],
                                 srcs=[src], dsts=[o for _, o in outs])

    def send(trs):
        g.remote_dma_fused(trs, local_sem=T.sem.ls)

    order = P["order"]
    place = dict([(s, 0)] + [(k, 1 + i) for i, k in enumerate(P["add"])])

    def xs(k, a, b):
        return T.xs[:, XS * k + a:XS * k + b]

    def of(k):
        return T.of[:, SL * place[k]:SL * place[k] + SL]

    def land(q, a, b):
        return T.land[:, Z0 + CAPP * q + a:Z0 + CAPP * q + b]

    def key(table):
        return [k for k, c in table.items() if c == core]

    target = s if is_rank else (key(P["pack"]) + [None])[0]
    second = (key(P["share"]) + [None])[0]
    expert = s if is_rank else (key(P["comp"]) + [second])[0]
    lead = not is_rank and expert is not None and second is None
    other = P["share"].get(expert) if lead else None
    parts = [] if expert is None else [1] if second is not None else [0] if other is not None else [0, 1]
    lo, hi = (PARTS[parts[0]][0], PARTS[parts[-1]][1]) if parts else (0, 0)
    n_sh = 1 + len(P["share"])
    told = [(0, 1), (1, n_sh), (n_sh, N - 1)]

    kc = {}
    if is_rank:
        m1 = tok(V.memset(T.pk[:, 8:9], -1))
        m2 = tok(V.memset(T.L[:, 8:12], 0.0))
        d1 = tok(g.sync.dma_start(T.pk[:, 0:8], T.pick[:, 0:64]), 16)
        d3 = tok(g.scalar.dma_start(T.L[:, 0:8], T.gate[:, 0:64]), 16)
        need("s", m1)
        d1 = also(d1, g.sync.dma_start(T.pk[0:32, 8:9], T.pick[:, 64:66]), 16)
        need("a", m2)
        d3 = also(d3, g.scalar.dma_start(T.L[0:32, 8:9], T.gate[:, 64:66]), 16)
        stg = []
        for b in range(NB):
            w = T.w1 if b < NB // 2 else T.w2
            c0 = (b % (NB // 2)) * WB
            stg.append(tok(g.sync.dma_start(T.wst[4 * b:4 * b + 4], w[:, c0:c0 + WB]), 16))
        XW = TOK // XC
        for i in range(XC):
            if i:
                g.sync.wait_ge(T.sem["go%d" % (i - 1)], 1)
            ins = g.sync.dma_start(T.xw[:, XW * i:XW * i + XW], T.x[:, XW * i:XW * i + XW])
            xl = also(xl, ins, 16) if i else tok(ins, 16)
        wl1 = tok(g.sync.dma_start(T.wsb[:, 0:512], T.w1[:]), 16)
        wl2 = tok(g.sync.dma_start(T.wsb[:, 512:1024], T.w2[:]), 16)
        wload = [wl1 if b < NB // 2 else wl2 for b in range(NB)]
        xz = tok(V.memset(T.xw[:, TOK:WIN], 0.0))

    c9 = {n: T.c9[:, 12 * i:12 * i + CH] for i, n in enumerate(_C9)}
    kc["o1"] = tok(V.memset(T.ones[:], 1.0))
    if target is not None:
        kc["z9"] = tok(V.memset(c9["z9"], 0.0))
        if is_rank:
            wz = tok(V.memset(T.win[:, 0:1024], 0.0))
        need("g", kc["o1"])
        kc["tri"] = tok(g.affine_select(T.tri[:], T.ones[:], [[1, 128]], A.is_gt, 0.0, 0, -1))
    kc["pp"] = tok(g.iota(T.pp[:, 0:SL], [[0, SL]], 0, 1))
    kc["ic"] = tok(g.iota(T.ic[:], [[-16, SL]], 0, 0, allow_small_or_imprecise_dtypes=True))
    kc["ia"] = tok(g.iota(T.ia[:], [[0, 8], [1, 16]], 1, 0, allow_small_or_imprecise_dtypes=True))
    if lead:
        kc["ids"] = tok(g.iota(T.ids[:], [[1, CAPP]], Z0, 0, allow_small_or_imprecise_dtypes=True))

    def pieces(b):
        hs = [c for c in P["hel"] if (b, c) in P["fwd"]]
        return hs, (4 if len(hs) <= 4 else 2)

    if is_rank:
        need("v", m1, d1)
        pfc = tok(V.tensor_copy(T.L[:, 12:21], T.pk[:, 0:CH]))
        lists = [pfc, d3, m2]
        need("g", *lists)
        hs = [P["pack"][r] for r in P["rot"]]
        send([transfer(T.L[:, 0:21], [(c, T.L[:, 0:21]) for c in hs], "lst", chip_bits)])
        for b in range(NB):
            need("g", stg[b])
            hs, ne = pieces(b)
            send([transfer(T.wst[4 * b + P["fwd"][b, c][0]], [(c, T.pc[b])], "pc%d" % b,
                           chip_bits[ne * j:ne * j + ne]) for j, c in enumerate(hs)])
            if b < XC - 1:
                g.sem_inc(T.sem["go%d" % b], 1)
        need("g", kc["tri"], kc["pp"], kc["ic"], kc["ia"])
        for i in range(2):
            for a, (p0, p1) in enumerate(SETS):
                ins = g.iota(T.idt[p0:p1, CAPP * i:CAPP * i + CAPP], [[1, CAPP]], Z0 + CAPP * (3 * i + a), 0,
                             allow_small_or_imprecise_dtypes=True)
                idt = also(idt, ins) if i or a else tok(ins)
                need("g", idt)

    def pad_constants():
        need("v", kc["pp"], kc["ic"])
        q1 = tok(V.tensor_scalar(T.pp[:, SL:2 * SL], T.pp[:, 0:SL], 15, None, A.bitwise_and))
        need("v", q1)
        kc["pm"] = tok(V.tensor_copy(T.pf2[:, 0:SL], T.pp[:, SL:2 * SL]))
        need("v", kc["pm"])
        if target is not None:
            q3 = tok(V.tensor_scalar(T.padc[:, 0:SL], T.ic[:], -1.0, float(TOK + 1), A.mult, A.add))
            need("v", q3)
            q4 = tok(V.tensor_tensor(T.padc[:, SL:2 * SL], T.pf2[:, 0:SL], T.padc[:, 0:SL], A.add))
            need("v", q4)
            kc["padc"] = tok(V.memset(T.padc[:, 0:SL], 0.0))

    def expert_constants():
        need("v", kc["ic"], kc["ia"], kc["pm"])
        kc["eo"] = tok(V.tensor_scalar(T.eo[:], T.ic[:], -1.0 / 16, None, A.mult))
        e1 = tok(V.tensor_scalar(T.pf2[:, SL:SL + 1], T.pf2[:, 0:1], 1.0, None, A.add))
        need("v", e1)
        for c in range(0, CAPP, 128):
            w = min(128, CAPP - c)
            ins = V.tensor_scalar(T.em[:, c:c + w], T.ia[:, 0:w], T.pf2[:, SL:SL + 1], None, A.is_equal)
            kc["em"] = also(kc["em"], ins) if c else tok(ins)

    pad_constants()
    if parts and not is_rank:
        expert_constants()

    def forward(blocks):
        for b in blocks:
            if (b, core) not in P["fwd"]:
                continue
            q, ranks = P["fwd"][b, core]
            via = {r: _relay(core, s, b, r, plans, cores, topo) for r in ranks}
            outs = ([(via[r][0], T.rl[via[r][1]]) for r in ranks if via[r] is not None]
                    + [(plans[r]["comp"][s], T.wland[4 * b + q]) for r in ranks if via[r] is None])
            g.wait_ge(T.sem["pc%d" % b], pieces(b)[1])
            send([transfer(T.pc[b], outs, _wsem(s, b, cores, topo), _wbits(core, b, outs[0][0], topo))])

    first = 1 if core in P["own"] else NB
    forward(range(first))

    if target is not None:
        r = target
        pf, gt = T.L[:, 12:21], T.L[:, 0:CH]
        if is_rank:
            need("v", *lists)
        else:
            V.wait_ge(T.sem.lst, nof)
        a1 = tok(V.tensor_scalar(c9["cl"], pf, float(TOK * r), float(TOK * r + TOK - 1), A.max, A.min))
        a2 = tok(V.tensor_scalar(c9["t2"], pf, float(-TOK * (r + 1)), None, A.add))
        need("v", a1)
        a3 = tok(V.tensor_tensor(c9["mk"], c9["cl"], pf, A.is_equal))
        need("v", a3, kc["z9"])
        a4 = tok(V.tensor_tensor_scan(c9["cum"], c9["mk"], c9["z9"], 0.0, A.add, A.add))
        need("p", a4, kc["tri"])
        a5 = tok(g.tensor.matmul(T.bb[:, 0:1], T.tri[:], c9["cum"][:, CH - 1:CH], True, True))
        need("v", a4, a5)
        a6 = tok(V.tensor_scalar(c9["s1u"], c9["cum"], T.bb[:, 0:1], None, A.add))
        need("v", a6)
        a7 = tok(V.tensor_tensor(c9["s1"], c9["s1u"], c9["mk"], A.mult))
        need("v", a7)
        a8 = tok(V.tensor_scalar(T.ci[:], c9["s1"], 1.0 / 16, 17.0 / 32, A.mult, A.subtract))
        need("v", a2)
        a9 = tok(V.tensor_tensor(c9["val"], c9["t2"], c9["s1"], A.subtract))
        need("v", a8)
        a10 = tok(V.tensor_scalar(c9["cf"], T.ci[:], -16.0, None, A.mult))
        need("v", a10)
        a11 = tok(V.tensor_tensor(c9["af"], c9["s1"], c9["cf"], A.add))
        need("v", a9, a11, kc["ia"], kc["ic"])
        for e in range(CH):
            rh = T.rh[:, 2 * SL * e:2 * SL * e + SL]
            rv = T.rh[:, 2 * SL * e + SL:2 * SL * e + 2 * SL]
            lh = T.lh[:, 128 * e:128 * e + 128]
            cfe, afe = c9["cf"][:, e:e + 1], c9["af"][:, e:e + 1]
            b1 = tok(V.tensor_scalar(rh, T.ic[:], cfe, gt[:, e:e + 1], A.is_equal, A.mult))
            if e in SCAL:
                dif = T.dif[:, 128 * e:128 * e + 128]
                need("a", a11, kc["ia"])
                need("a", tok(g.scalar.activation(dif, T.ia[:], F.Abs, afe, -1.0)))
                b1 = also(b1, g.scalar.activation(lh, dif, F.Relu, 1.0, -1.0))
            else:
                b1 = also(b1, V.tensor_scalar(lh, T.ia[:], afe, None, A.is_equal))
            b1 = also(b1, V.tensor_scalar(rv, T.ic[:], cfe, c9["val"][:, e:e + 1], A.is_equal, A.mult))
            need("p", b1)
            mm = g.tensor.matmul(T.cb[:, 0:2 * SL], lh, T.rh[:, 2 * SL * e:2 * SL * e + 2 * SL], e == 0, e == CH - 1)
            if e == CH - 1:
                cbt = tok(mm)
        need("v", cbt, kc["padc"])
        mg = tok(V.tensor_tensor(xs(s, CAPP, XS) if is_rank else T.msg[:], T.cb[:, 0:2 * SL], T.padc[:], A.add))
        if not is_rank:
            need("g", mg)
            to = plans[r]["comp"][s]
            send([transfer(T.msg[:], [(cores[r], xs(s, CAPP, XS)), (to, T.xk[:, CAPP:XS])], "msg%d" % s,
                           _bits(topo.mask(core, cores[r])))])

    def packed(k):
        V.wait_ge(T.sem["msg%d" % k], len(_bits(topo.mask(plans[k]["pack"][s], R))))

    forward(range(first, NB))

    if lead:
        me = place[expert]
        wz = tok(V.memset(T.win[:, 0:WIN], 0.0))
        need("v", kc["ids"], kc["ia"])
        for q in range(1, me):
            ins = V.tensor_scalar(T.idt[:, CAPP * q:CAPP * q + CAPP], T.ids[:], float(CAPP * q), None, A.add)
            idt = also(idt, ins) if q > 1 else tok(ins)
        for c in range(0, CAPP, 128):
            w = min(128, CAPP - c)
            ins = V.tensor_scalar(T.rm[:, c:c + w], T.ia[:, 0:w], 1.0, None, A.is_gt)
            kc["rm"] = also(kc["rm"], ins) if c else tok(ins)

    def factors(src):
        need("v", kc["eo"], kc["em"])
        tg = tok(V.tensor_tensor(T.tmpg[:, lo:hi], src.indirect(T.eo[:, lo // 16:hi // 16]), T.em[:, lo:hi], A.mult))
        need("p", tg, kc["o1"])
        gm = tok(g.tensor.matmul(T.gb[:, lo:hi], T.ones[0:16, 0:128], T.tmpg[0:16, lo:hi], True, True))
        need("a", gm)
        return tok(g.scalar.activation(T.gs[:, lo:hi], T.gb[:, lo:hi], F.Copy))

    if is_rank:
        offs = {}

        def offsets(k):
            offs[k] = tok(V.tensor_copy(of(k), xs(k, CAPP + SL, XS)))

        def tell(i):
            q0, q1 = told[i]
            hs = [P["comp"][x] for x in order if place[x] > q0]
            need("g", *[offs[k] for k in offs if q0 <= place[k] < q1])
            lot = T.of[:, SL * q0:SL * q1]
            send([transfer(lot, [(c, lot) for c in hs], "of%d" % i, chip_bits)])

        def gather(k, q):
            need(q, offs[k], xz, xl)
            src = T.xw[:, 0:WIN].indirect(of(k))
            return tok(V.tensor_copy(xs(k, 0, CAPP), src) if q == "v"
                       else g.scalar.activation(xs(k, 0, CAPP), src, F.Copy))

        expert_constants()
        zz = tok(V.memset(T.land[:, 0:Z0], 0.0))
        need("v", mg)
        offsets(s)
        tell(0)
        gc = factors(xs(s, CAPP, CAPP + SL))
        wz = also(wz, V.memset(T.win[:, 1024:16 * ROW], 0.0))
        xown = gather(s, "v")
        half = XS - PARTS[1][0]
        for i, k in enumerate(order):
            packed(k)
            offsets(k)
            need("g", gather(k, "av"[i % 2]))
            c = P["comp"][k]
            if k in P["share"]:
                send([transfer(xs(k, 0, half), [(c, T.xk[:, 0:half])], "xin", chip_bits[:nof // 2]),
                      transfer(xs(k, XS - half, XS), [(P["share"][k], T.xk[:, XS - half:XS])], "xin",
                               chip_bits[nof // 2:])])
            else:
                send([transfer(xs(k, 0, CAPP), [(c, T.xk[:, 0:CAPP])], "xin", chip_bits)])
            if k == order[-1]:
                tell(1)
            elif i == N - 2 - len(P["share"]):
                tell(2)
        need("v", *offs.values())
        step(V.tensor_copy(T.oi[:], T.of[:]))
        step(V.tensor_scalar(T.oh[:], T.oi[:], 4, None, A.arith_shift_right))
        step(V.tensor_scalar(T.oa[:], T.oi[:], float(ROW), None, A.mult), False)
        step(V.tensor_scalar(T.ob[:], T.oh[:], float(1 - 16 * ROW), None, A.mult))
        step(V.tensor_tensor(T.oc[:], T.oa[:], T.ob[:], A.add))
        for i in range(2):
            for a, (p0, p1) in enumerate(SETS):
                step(V.tensor_copy(T.op[p0:p1, SL * i:SL * i + SL],
                                   T.oc[p0:p1, SL * (3 * i + a):SL * (3 * i + a + 1)]), i == 1 and a == 2)
        need("v", idt, wz)
        for i in range(2):
            step(V.tensor_copy(T.win[:].indirect(T.op[:, SL * i:SL * i + SL]), T.idt[:, CAPP * i:CAPP * i + CAPP]))
        g.sync.wait_ge(T.sem.lk, steps[0])
        for a in range(3):
            ins = g.sync.dma_start(T.iv[:, ROW * a:ROW * a + ROW], T.win[32 * a:32 * a + 8, :])
            ivt = also(ivt, ins, 16) if a else tok(ins, 16)

    def make_prev():
        need("v", wz, kc["ids"])
        for q in range(me):
            for i, (q0, _) in enumerate(told):
                if q0 == q:
                    V.wait_ge(T.sem["of%d" % i], nof)
            if q:
                need("v", idt)
            ids = T.idt[:, CAPP * q:CAPP * q + CAPP] if q else T.ids[:]
            need("v", tok(V.tensor_copy(T.win[:, 0:WIN].indirect(T.of[:, SL * q:SL * q + SL]), ids)))
        need("v", oq, kc["em"], kc["rm"])
        p1 = tok(V.tensor_tensor(T.pg[:], T.win[:, 0:WIN].indirect(T.oq[:, 0:SL]), T.em[:], A.mult))
        need("v", p1)
        p2 = tok(V.tensor_tensor_scan(T.ps[:], T.rm[:], T.pg[:], 0.0, A.mult, A.add))
        need("v", p2)
        need("g", tok(V.tensor_copy(T.pv[:], T.ps[:, 15:CAPP:16])))
        send([transfer(T.pv[:], [(R, T.pvl[:, SL * me:SL * me + SL])], "pv%d" % me, chip_bits)])

    def first_layer():
        hs = []
        for f in range(4):
            need("p", wload[128 * f // WB])
            ht = tok(g.tensor.matmul(T["h%d" % f][:, lo:hi], T.wsb[:, 128 * f:128 * f + 128], xb[:, lo:hi], True, True))
            need("a", ht)
            hs.append(tok(g.scalar.activation(T.hid[:, CAPP * f + lo:CAPP * f + hi], T["h%d" % f][:, lo:hi], F.Relu)))
        return hs

    if is_rank:
        xb = xs(s, 0, XS)
        need("p", xown)
        hid = first_layer()
    elif lead:
        xb = T.xk
        wload = []
        for b in range(NB):
            tot = 0
            for (b2, c), (q, ranks) in plans[expert]["fwd"].items():
                if b2 == b and s in ranks:
                    v = _relay(c, expert, b, s, plans, cores, topo)
                    tot += len(_wbits(c, b, core, topo)) if v is None else len(_bits(topo.mask(v[0], core)))
            g.sync.wait_ge(T.sem[_wsem(expert, b, cores, topo)], tot)
            wload.append(tok(g.sync.dma_start(T.wsb[:, WB * b:WB * b + WB], T.wland[4 * b:4 * b + 4]), 16))
            if other is not None:
                need("g", wload[b])
                send([transfer(T.wsb[:, WB * b:WB * b + WB], [(other, T.wsb[:, WB * b:WB * b + WB])], "wx%d" % b,
                               chip_bits)])
        packed(expert)
        oq = tok(V.tensor_copy(T.oq[:], T.xk[:, CAPP + SL:XS]))
        gc = factors(T.xk[:, CAPP:CAPP + SL])
        make_prev()
        g.tensor.wait_ge(T.sem.xin, nof if other is None else nof // 2)
        hid = first_layer()
    elif second is not None:
        xb = T.xk
        wload = [("wx%d" % b, nof) for b in range(NB)]
        g.tensor.wait_ge(T.sem.xin, nof // 2)
        hid = first_layer()
        V.wait_ge(T.sem.xin, nof // 2)
        gc = factors(T.xk[:, CAPP:CAPP + SL])
    ybank = [T.y0, T.bb]
    yt = {}
    for f in range(4 if parts else 0):
        need("p", wload[(512 + 128 * f) // WB], hid[f])
        for h in parts:
            p0, p1 = PARTS[h]
            mm = g.tensor.matmul(ybank[h][:, 0:p1 - p0], T.wsb[:, 512 + 128 * f:640 + 128 * f],
                                 T.hid[:, CAPP * f + p0:CAPP * f + p1], f == 0, f == 3)
            if f == 3:
                yt[h] = tok(mm)
    for h in parts:
        p0, p1 = PARTS[h]
        need("v", yt[h], gc)
        if is_rank:
            own_res = V.tensor_tensor(land(0, p0, p1), ybank[h][:, 0:p1 - p0], T.gs[:, p0:p1], A.mult)
            ownt = also(ownt, own_res) if h else tok(own_res)
        else:
            need("g", tok(V.tensor_tensor(T.res[:, p0:p1], ybank[h][:, 0:p1 - p0], T.gs[:, p0:p1], A.mult)))
            send([transfer(T.res[:, p0:p1], [(R, land(place[expert], p0, p1))],
                           "res%d_%d" % (place[expert], h), chip_bits)])

    if is_rank:
        need("v", ivt)
        step(V.tensor_tensor(T.im[:, 0:256], T.iv[:, 0:256], T.iv[:, ROW:ROW + 256], A.max))
        step(V.tensor_tensor(T.im[:, 256:512], T.im[:, 0:256], T.iv[:, 2 * ROW:2 * ROW + 256], A.max))
        step(V.tensor_copy(T.inv[:], T.im[:, 256:512]))
        n = 0
        need("v", zz, ownt)
        for q in range(1, N):
            V.wait_ge(T.sem["pv%d" % q], nof)
            for h, (p0, p1) in enumerate(PARTS):
                V.wait_ge(T.sem["res%d_%d" % (q, h)], nof)
                off = T.pvl[:, SL * q + p0 // 16:SL * q + p1 // 16]
                V.tensor_tensor(land(q, p0, p1), T.land[:, 0:Z0 + CAPP * q].indirect(off), land(q, p0, p1),
                                A.add).then_inc(T.sem.sum, 1)
                n += 1
            V.wait_ge(T.sem.sum, n)
        g.scalar.wait_ge(T.sem.sum, n)
        g.scalar.wait_ge(T.sem.lk, steps[0])
        yd = None
        for a, b, q in YP:
            src = T.land[:].indirect(T.inv[:, a // 16:b // 16])
            need("s", tok(V.tensor_copy(T.yb[:, a:b], src) if q == "v"
                          else g.scalar.activation(T.yb[:, a:b], src, F.Copy)))
            ins = g.sync.dma_start(T.y[:, a:b], T.yb[:, a:b])
            yd = also(yd, ins, 16) if yd else tok(ins, 16)
        need("s", yd)

    if nls[0]:
        g.wait_ge(T.sem.ls, nls[0])
